import numpy as np
import ml_dtypes


def mxq(x, axis, fmt="e4m3"):
    dtype, down = {"e4m3": (ml_dtypes.float8_e4m3fn, 7), "e5m2": (ml_dtypes.float8_e5m2, 14)}[fmt]
    v = np.moveaxis(np.asarray(x, np.float32).astype(ml_dtypes.bfloat16).astype(np.float64), axis, -1)
    blocks = v.reshape(v.shape[:-1] + (-1, 32))
    amax = np.abs(blocks).max(-1, keepdims=True)
    byte = np.maximum(np.where(amax > 0, np.frexp(amax)[1] - 1 + 127, 0) - down, 1)
    scale = np.exp2(byte - 127.0)
    codes = (blocks / scale).astype(np.float32).astype(dtype).astype(np.float64)
    return np.moveaxis((codes * scale).reshape(v.shape), -1, axis)


WIDE = False


def mx_kscale(k):
    if not WIDE:
        return np.ones(k)
    levels = np.array([10, -10, 5, -5, 0])
    if k % 512:
        return np.exp2(np.random.permutation(np.resize(levels, k // 32))).repeat(32)
    a = np.empty((k // 512, 16))
    for p in range(k // 512):
        a[p, :8] = np.random.permutation(np.resize(levels, 8))
        for g in range(8):
            far = levels[np.abs(levels - a[p, g]) >= 10]
            a[p, g + 8] = far[np.random.randint(len(far))]
    return np.exp2(a.ravel()).repeat(32)


def f64(x):
    return np.asarray(x).astype(np.float64)


def striped(idx):
    return np.tile(idx.reshape(-1, 16).T, (8, 1)).astype(np.uint16)


def unstriped(offs):
    return offs[:16].T.reshape(-1).astype(np.int64)


E2M1 = np.array([0.0, 0.5, 1.0, 1.5, 2.0, 3.0, 4.0, 6.0, -0.0, -0.5, -1.0, -1.5, -2.0, -3.0, -4.0, -6.0])


def pack_weight(w, fmt):
    k, n = w.shape
    w = f64(np.asarray(w, np.float32).astype(ml_dtypes.bfloat16)).reshape(k // 32, 32, n)
    amax = np.abs(w).max(1)
    if fmt == "e4m3":
        byte = np.frexp(amax)[1] - 1 + 127 - 7
    else:
        mant, ex = np.frexp(amax / 6.0)
        byte = np.where(mant > 0.5, ex, ex - 1) + 127
    byte = np.clip(np.where(amax > 0, byte, 1), 1, 254)
    scaled = (w * np.exp2(127.0 - byte)[:, None, :]).reshape(k, n).astype(np.float32)
    by_word = np.ascontiguousarray(scaled.reshape(k // 512, 128, 4, n).transpose(0, 1, 3, 2))
    if fmt == "e4m3":
        words = by_word.astype(ml_dtypes.float8_e4m3fn).view(np.uint8)
    else:
        c = by_word.astype(ml_dtypes.float4_e2m1fn).view(np.uint8) & 0xF
        words = (c[..., 0::2] | (c[..., 1::2] << 4)).reshape(k // 512, 128, 2 * n)
    return np.ascontiguousarray(words), np.ascontiguousarray(byte.astype(np.uint8).reshape(k // 512, 16, n))


def unpack_weight(words, scales, fmt):
    g, _, n = scales.shape
    words = np.ascontiguousarray(words).reshape(g, 128, n, -1)
    if fmt == "e4m3":
        vals = words.view(ml_dtypes.float8_e4m3fn).astype(np.float64)
    else:
        nib = np.empty((g, 128, n, 4), np.uint8)
        nib[..., 0::2] = words & 0xF
        nib[..., 1::2] = words >> 4
        vals = E2M1[nib]
    vals = vals * np.repeat(np.exp2(scales.astype(np.float64) - 127.0), 8, axis=1)[..., None]
    return vals.transpose(0, 1, 3, 2).reshape(g * 512, n)


def split(x):
    m, e = np.frexp(f64(x))
    hi = np.ldexp(np.trunc(16.0 * m) / 16.0, e)
    return hi, f64(x) - hi


K, M, T, S = 512, 256, 4096, 1536


def setup_inputs():
    n = np.random.standard_normal
    s = mx_kscale(K)[:, None]
    v = pack_weight(n((K, T)) * s, "e4m3")
    return {
        "tab_words": v[0],
        "tab_scales": v[1],
        "w": (n((K, M)) / np.sqrt(K) / s).astype(np.float32),
        "ts": np.tile(np.exp(0.5 * n(T)), (128, 1)).astype(np.float32),
        "b": (0.3 * n(256)).astype(np.float32),
        "offs": striped(np.random.permutation(T)[:S]),
    }


def reference(tab_words, tab_scales, w, ts, b, offs):
    tab_ = unpack_weight(tab_words, tab_scales, "e4m3")[:, unstriped(offs)]
    w_hi, w_lo = split(w)
    w_hi_, w_lo_ = mxq(w_hi, 0, "e4m3"), mxq(w_lo, 0, "e4m3")
    y = w_hi_.T @ tab_ + w_lo_.T @ tab_
    y = y * f64(ts)[0][unstriped(offs)]
    return y + f64(b)[:, None]

@@ -1,0 +1,178 @@
+from contextlib import ExitStack
+
+import concourse.mybir as mybir
+
+K, M, T, S = 512, 256, 4096, 1536
+FLOPS = 2 * 2 * K * M * S
+
+F32 = mybir.dt.float32
+BF16 = mybir.dt.bfloat16
+I32 = mybir.dt.int32
+U32 = mybir.dt.uint32
+U16 = mybir.dt.uint16
+U8 = mybir.dt.uint8
+FP8X4 = mybir.dt.float8_e4m3fn_x4
+ALU = mybir.AluOpType
+ACT = mybir.ActivationFunctionType
+
+P = 128
+PACK = 4
+SLICE = 512
+SLICES = S // SLICE
+TILES = SLICE // P
+HI_MASK = -(1 << 20)
+RUN = T // P
+QUAD = 4
+
+
+def tile_list_tabts_bias_kernel(tc, tab_words, tab_scales, w, ts, b, offs, out):
+    nc = tc.nc
+    with ExitStack() as ctx:
+        keep = ctx.enter_context(tc.tile_pool(name="keep", bufs=1))
+        ring = ctx.enter_context(tc.tile_pool(name="ring", bufs=8))
+        stage = ctx.enter_context(tc.tile_pool(name="stage", bufs=6))
+        psum = ctx.enter_context(tc.psum_pool(name="psum", bufs=2))
+
+        offsets = keep.tile([P, S // 16], U16, name="offsets")
+        nc.sync.dma_start(offsets[:], offs)
+
+        ts_runs = keep.tile([P, RUN], F32, name="ts_runs")
+        nc.sync.dma_start(ts_runs[:], ts[0].rearrange("(p c) -> p c", c=RUN))
+
+        scale_win = keep.tile([P, T // 4], I32, name="scale_win", align_bytes=64)
+        nc.vector.memset(scale_win[:], 0)
+
+        zeros = keep.tile([P, P], F32, name="zeros", tag="early_late", align_bytes=64)
+        nc.vector.memset(zeros[:], 0.0)
+        ident = keep.tile([P, P], F32, name="ident")
+        nc.gpsimd.affine_select(
+            out=ident[:], in_=zeros[:], pattern=[[-1, P]], compare_op=ALU.not_equal, fill=1.0, base=0, channel_multiplier=1
+        )
+
+        w_raw = keep.tile([P, PACK, M], F32, name="w_raw", align_bytes=64)
+        nc.sync.dma_start(w_raw[:], w.rearrange("(p t) n -> p t n", t=PACK))
+
+        scale_rows = tab_scales[0].bitcast(I32)
+        for r in range(4):
+            nc.sync.dma_start(scale_win[r:P:32, :], scale_rows[r:16:4, :])
+
+        word_win = keep.tile([P, T], I32, name="word_win", tag="early_late", align_bytes=64)
+        nc.sync.dma_start(word_win[:], tab_words[0].rearrange("p t i -> p (t i)").bitcast(I32))
+
+        b_col = keep.tile([P, M // P], F32, name="b_col")
+        with nc.allow_non_contiguous_dma(reason="one bias value to a partition"):
+            nc.sync.dma_start(b_col[:], b.rearrange("(m p) -> p m", p=P))
+
+        words = [keep.tile([P, SLICE], U32, name="words%d" % s, align_bytes=64) for s in range(SLICES)]
+        scales = [keep.tile([P, SLICE], U8, name="scales%d" % s, align_bytes=64) for s in range(SLICES)]
+        ts_g = [keep.tile([P, SLICE], F32, name="ts_g%d" % s, align_bytes=64) for s in range(SLICES)]
+
+        def list_slice(s):
+            return offsets[:, s * (SLICE // 16) : (s + 1) * (SLICE // 16)]
+
+        def gather_scales(s):
+            nc.vector.tensor_copy(scales[s][:], scale_win[:].bitcast(U8).indirect(list_slice(s)))
+
+        def gather_words(s):
+            nc.vector.tensor_copy(words[s][:], word_win[:].bitcast(U32).indirect(list_slice(s)))
+
+        def gather_ts(s):
+            nc.vector.tensor_copy(ts_g[s][:], ts_win[:].indirect(list_slice(s)))
+
+        w_grouped = w_raw[:].rearrange("p t n -> p n t")
+        w_hi = keep.tile([P, M, PACK], I32, name="w_hi", align_bytes=64)
+        parts = keep.tile([P, 2, M, PACK], BF16, name="parts", align_bytes=64)
+        w_codes = keep.tile([P, 2 * M], U32, name="w_codes", align_bytes=64)
+        w_scales = keep.tile([P, 2 * M], U8, name="w_scales", align_bytes=64)
+
+        nc.vector.tensor_scalar(
+            w_hi[:], w_raw[:].bitcast(I32).rearrange("p t n -> p n t"), HI_MASK, None, ALU.bitwise_and
+        )
+        nc.scalar.activation(parts[:, 0, :, :], w_hi[:].bitcast(F32), ACT.Copy)
+
+        ts_win = keep.tile([P, T], F32, name="ts_win", align_bytes=64)
+        ts_cells = ts_win[:].rearrange("m (p c) -> m p c", c=RUN)
+        for q in range(RUN // QUAD):
+            spread = psum.tile([P, QUAD, P], F32, name="spread", tag="ts_bank")
+            for i in range(QUAD):
+                c = q * QUAD + i
+                nc.tensor.transpose(spread[:, i, :], ts_runs[:, c : c + 1].to_broadcast([P, P]), ident[:])
+            nc.scalar.activation(
+                ts_cells[:, :, q * QUAD : (q + 1) * QUAD], spread[:].rearrange("m c p -> m p c"), ACT.Copy
+            )
+
+        gather_scales(0)
+        nc.vector.tensor_tensor(parts[:, 1, :, :], w_grouped, w_hi[:].bitcast(F32), ALU.subtract)
+        gather_scales(1)
+        nc.vector.quantize_mx(
+            out=w_codes[:].bitcast(FP8X4), scales=w_scales[:], in_=parts[:].rearrange("p h n t -> p (h n t)")
+        )
+        gather_scales(2)
+
+        def finish(source, s, m):
+            rows = slice(m * P, (m + 1) * P)
+            result = stage.tile([P, SLICE], F32, name="result")
+            nc.scalar.activation(result[:], source[:], ACT.Identity, bias=b_col[:, m : m + 1])
+            nc.sync.dma_start(out[rows, s * SLICE : (s + 1) * SLICE], result[:])
+
+        def project_turned(s):
+            turned = psum.tile([P, TILES, P], F32, name="turned", tag="ts_bank")
+            for i in range(TILES):
+                nc.tensor.transpose(turned[:, i, :], ts_g[s][:, i * P : (i + 1) * P], ident[:])
+            ts_col = ring.tile([P, TILES], F32, name="ts_col")
+            nc.scalar.activation(ts_col[:], turned[:, :, 0], ACT.Copy)
+            scaled = []
+            for i in range(TILES):
+                cols = slice(i * P, (i + 1) * P)
+                y = psum.tile([P, M], F32, name="y", tag="y_bank", bufs=4)
+                for h in range(2):
+                    nc.tensor.matmul_mx(
+                        out=y[:],
+                        lhsT=words[s][:, cols].bitcast(FP8X4),
+                        lhsT_scale=scales[s][:, cols],
+                        rhs=w_codes[:, h * M : (h + 1) * M].bitcast(FP8X4),
+                        rhs_scale=w_scales[:, h * M : (h + 1) * M],
+                        start=(h == 0),
+                        stop=(h == 1),
+                    )
+                z = ring.tile([P, M], F32, name="z")
+                nc.scalar.activation(z[:], y[:], ACT.Copy, scale=ts_col[:, i : i + 1])
+                scaled.append(z)
+            for m in range(M // P):
+                back = psum.tile([P, SLICE], F32, name="back", tag="back_bank")
+                for i in range(TILES):
+                    nc.tensor.transpose(back[:, i * P : (i + 1) * P], scaled[i][:, m * P : (m + 1) * P], ident[:])
+                finish(back, s, m)
+
+        def project_direct(s):
+            for m in range(M // P):
+                y = psum.tile([P, SLICE], F32, name="y", tag="y_bank", bufs=4)
+                for h in range(2):
+                    cols = slice(h * M + m * P, h * M + (m + 1) * P)
+                    nc.tensor.matmul_mx(
+                        out=y[:],
+                        lhsT=w_codes[:, cols].bitcast(FP8X4),
+                        lhsT_scale=w_scales[:, cols],
+                        rhs=words[s][:].bitcast(FP8X4),
+                        rhs_scale=scales[s][:],
+                        start=(h == 0),
+                        stop=(h == 1),
+                    )
+                z = stage.tile([P, SLICE], F32, name="zd")
+                nc.vector.tensor_tensor(z[:], y[:], ts_g[s][:], ALU.mult)
+                if s == SLICES - 1 and m == M // P - 1:
+                    result = stage.tile([P, SLICE], F32, name="result")
+                    nc.vector.tensor_scalar(result[:], z[:], b_col[:, m : m + 1], None, ALU.add)
+                    nc.sync.dma_start(out[m * P : (m + 1) * P, s * SLICE : (s + 1) * SLICE], result[:])
+                else:
+                    finish(z, s, m)
+
+        gather_words(0)
+        gather_ts(0)
+        project_turned(0)
+        gather_words(1)
+        gather_ts(1)
+        project_turned(1)
+        gather_words(2)
+        gather_ts(2)
+        project_direct(2)

@@ -21,7 +21,9 @@ SLICE = 512
 SLICES = S // SLICE
 TILES = SLICE // P
 HI_MASK = -(1 << 20)
-RUN = T // P
+TS_TAIL = 2048
+TS_HEAD = T - TS_TAIL
+RUN = TS_HEAD // P
 QUAD = 4
 
 
@@ -29,20 +31,19 @@ def tile_list_tabts_bias_kernel(tc, tab_words, tab_scales, w, ts, b, offs, out):
     nc = tc.nc
     with ExitStack() as ctx:
         keep = ctx.enter_context(tc.tile_pool(name="keep", bufs=1))
-        ring = ctx.enter_context(tc.tile_pool(name="ring", bufs=8))
+        windows = ctx.enter_context(tc.tile_pool(name="windows", bufs=1))
         stage = ctx.enter_context(tc.tile_pool(name="stage", bufs=6))
-        psum = ctx.enter_context(tc.psum_pool(name="psum", bufs=2))
+        psum = ctx.enter_context(tc.psum_pool(name="psum", bufs=8))
 
         offsets = keep.tile([P, S // 16], U16, name="offsets")
-        nc.sync.dma_start(offsets[:], offs)
 
         ts_runs = keep.tile([P, RUN], F32, name="ts_runs")
-        nc.sync.dma_start(ts_runs[:], ts[0].rearrange("(p c) -> p c", c=RUN))
+        nc.sync.dma_start(ts_runs[:], ts[0, :TS_HEAD].rearrange("(p c) -> p c", c=RUN))
 
         scale_win = keep.tile([P, T // 4], I32, name="scale_win", align_bytes=64)
         nc.vector.memset(scale_win[:], 0)
 
-        zeros = keep.tile([P, P], F32, name="zeros", tag="early_late", align_bytes=64)
+        zeros = windows.tile([P, P], F32, name="zeros", align_bytes=64, offset=4 * T - 256)
         nc.vector.memset(zeros[:], 0.0)
         ident = keep.tile([P, P], F32, name="ident")
         nc.gpsimd.affine_select(
@@ -52,18 +53,25 @@ def tile_list_tabts_bias_kernel(tc, tab_words, tab_scales, w, ts, b, offs, out):
         w_raw = keep.tile([P, PACK, M], F32, name="w_raw", align_bytes=64)
         nc.sync.dma_start(w_raw[:], w.rearrange("(p t) n -> p t n", t=PACK))
 
+        nc.sync.dma_start(offsets[:], offs)
+
         scale_rows = tab_scales[0].bitcast(I32)
         for r in range(4):
             nc.sync.dma_start(scale_win[r:P:32, :], scale_rows[r:16:4, :])
 
-        word_win = keep.tile([P, T], I32, name="word_win", tag="early_late", align_bytes=64)
-        nc.sync.dma_start(word_win[:], tab_words[0].rearrange("p t i -> p (t i)").bitcast(I32))
+        word_win = windows.tile([P, T], I32, name="word_win", align_bytes=64, offset=0)
+        word_rows = tab_words[0].rearrange("p t i -> p (t i)").bitcast(I32)
+        for c0 in range(0, T, T // 1):
+            nc.sync.dma_start(word_win[:, c0 : c0 + T // 1], word_rows[:, c0 : c0 + T // 1])
 
-        b_col = keep.tile([P, M // P], F32, name="b_col")
+        ts_win = windows.tile([P, T], F32, name="ts_win", align_bytes=64, offset=4 * T + 64)
+        nc.sync.dma_start(ts_win[:, TS_HEAD:], ts[:, TS_HEAD:])
+
+        b_col = windows.tile([P, M // P], F32, name="b_col", align_bytes=64, offset=4 * T)
         with nc.allow_non_contiguous_dma(reason="one bias value to a partition"):
             nc.sync.dma_start(b_col[:], b.rearrange("(m p) -> p m", p=P))
 
-        words = [keep.tile([P, SLICE], U32, name="words%d" % s, align_bytes=64) for s in range(SLICES)]
+        words = {}
         scales = [keep.tile([P, SLICE], U8, name="scales%d" % s, align_bytes=64) for s in range(SLICES)]
         ts_g = [keep.tile([P, SLICE], F32, name="ts_g%d" % s, align_bytes=64) for s in range(SLICES)]
 
@@ -73,7 +81,8 @@ def tile_list_tabts_bias_kernel(tc, tab_words, tab_scales, w, ts, b, offs, out):
         def gather_scales(s):
             nc.vector.tensor_copy(scales[s][:], scale_win[:].bitcast(U8).indirect(list_slice(s)))
 
-        def gather_words(s):
+        def gather_words(s, tag):
+            words[s] = keep.tile([P, SLICE], U32, name="words%d" % s, tag=tag, align_bytes=64)
             nc.vector.tensor_copy(words[s][:], word_win[:].bitcast(U32).indirect(list_slice(s)))
 
         def gather_ts(s):
@@ -88,91 +97,87 @@ def tile_list_tabts_bias_kernel(tc, tab_words, tab_scales, w, ts, b, offs, out):
         nc.vector.tensor_scalar(
             w_hi[:], w_raw[:].bitcast(I32).rearrange("p t n -> p n t"), HI_MASK, None, ALU.bitwise_and
         )
-        nc.scalar.activation(parts[:, 0, :, :], w_hi[:].bitcast(F32), ACT.Copy)
 
-        ts_win = keep.tile([P, T], F32, name="ts_win", align_bytes=64)
-        ts_cells = ts_win[:].rearrange("m (p c) -> m p c", c=RUN)
+        ts_cells = ts_win[:, :TS_HEAD].rearrange("m (p c) -> m p c", c=RUN)
         for q in range(RUN // QUAD):
-            spread = psum.tile([P, QUAD, P], F32, name="spread", tag="ts_bank")
+            spread = psum.tile([P, QUAD, P], F32, name="spread", tag="bank")
             for i in range(QUAD):
                 c = q * QUAD + i
                 nc.tensor.transpose(spread[:, i, :], ts_runs[:, c : c + 1].to_broadcast([P, P]), ident[:])
             nc.scalar.activation(
                 ts_cells[:, :, q * QUAD : (q + 1) * QUAD], spread[:].rearrange("m c p -> m p c"), ACT.Copy
             )
+            if q == 0:
+                nc.scalar.activation(parts[:, 0, :, :], w_hi[:].bitcast(F32), ACT.Copy)
 
         gather_scales(0)
-        nc.vector.tensor_tensor(parts[:, 1, :, :], w_grouped, w_hi[:].bitcast(F32), ALU.subtract)
+        nc.gpsimd.tensor_tensor(parts[:, 1, :, :], w_grouped, w_hi[:].bitcast(F32), ALU.subtract)
         gather_scales(1)
         nc.vector.quantize_mx(
             out=w_codes[:].bitcast(FP8X4), scales=w_scales[:], in_=parts[:].rearrange("p h n t -> p (h n t)")
         )
         gather_scales(2)
 
-        def finish(source, s, m):
-            rows = slice(m * P, (m + 1) * P)
+        sums = {}
+        scaled = {}
+
+        def project(s, m):
+            y = psum.tile([P, SLICE], F32, name="y", tag="bank")
+            for h in range(2):
+                cols = slice(h * M + m * P, h * M + (m + 1) * P)
+                nc.tensor.matmul_mx(
+                    out=y[:],
+                    lhsT=w_codes[:, cols].bitcast(FP8X4),
+                    lhsT_scale=w_scales[:, cols],
+                    rhs=words[s][:].bitcast(FP8X4),
+                    rhs_scale=scales[s][:],
+                    start=(h == 0),
+                    stop=(h == 1),
+                )
+            sums[s, m] = y
+
+        def evacuate(s, m):
+            y_out = keep.tile([P, SLICE], F32, name="y_out", tag="y_out%d%d" % (s, m), align_bytes=64)
+            nc.scalar.activation(y_out[:], sums[s, m][:], ACT.Copy)
+            sums[s, m] = y_out
+
+        def scale(engine, s, m):
+            z = stage.tile([P, SLICE], F32, name="z")
+            engine.tensor_tensor(z[:], sums[s, m][:], ts_g[s][:], ALU.mult)
+            scaled[s, m] = z
+
+        def finish(on_vector, s, m):
             result = stage.tile([P, SLICE], F32, name="result")
-            nc.scalar.activation(result[:], source[:], ACT.Identity, bias=b_col[:, m : m + 1])
-            nc.sync.dma_start(out[rows, s * SLICE : (s + 1) * SLICE], result[:])
+            if on_vector:
+                nc.vector.tensor_scalar(result[:], scaled[s, m][:], b_col[:, m : m + 1], None, ALU.add)
+            else:
+                nc.scalar.activation(result[:], scaled[s, m][:], ACT.Identity, bias=b_col[:, m : m + 1])
+            nc.sync.dma_start(out[m * P : (m + 1) * P, s * SLICE : (s + 1) * SLICE], result[:])
 
-        def project_turned(s):
-            turned = psum.tile([P, TILES, P], F32, name="turned", tag="ts_bank")
-            for i in range(TILES):
-                nc.tensor.transpose(turned[:, i, :], ts_g[s][:, i * P : (i + 1) * P], ident[:])
-            ts_col = ring.tile([P, TILES], F32, name="ts_col")
-            nc.scalar.activation(ts_col[:], turned[:, :, 0], ACT.Copy)
-            scaled = []
-            for i in range(TILES):
-                cols = slice(i * P, (i + 1) * P)
-                y = psum.tile([P, M], F32, name="y", tag="y_bank", bufs=4)
-                for h in range(2):
-                    nc.tensor.matmul_mx(
-                        out=y[:],
-                        lhsT=words[s][:, cols].bitcast(FP8X4),
-                        lhsT_scale=scales[s][:, cols],
-                        rhs=w_codes[:, h * M : (h + 1) * M].bitcast(FP8X4),
-                        rhs_scale=w_scales[:, h * M : (h + 1) * M],
-                        start=(h == 0),
-                        stop=(h == 1),
-                    )
-                z = ring.tile([P, M], F32, name="z")
-                nc.scalar.activation(z[:], y[:], ACT.Copy, scale=ts_col[:, i : i + 1])
-                scaled.append(z)
-            for m in range(M // P):
-                back = psum.tile([P, SLICE], F32, name="back", tag="back_bank")
-                for i in range(TILES):
-                    nc.tensor.transpose(back[:, i * P : (i + 1) * P], scaled[i][:, m * P : (m + 1) * P], ident[:])
-                finish(back, s, m)
-
-        def project_direct(s):
-            for m in range(M // P):
-                y = psum.tile([P, SLICE], F32, name="y", tag="y_bank", bufs=4)
-                for h in range(2):
-                    cols = slice(h * M + m * P, h * M + (m + 1) * P)
-                    nc.tensor.matmul_mx(
-                        out=y[:],
-                        lhsT=w_codes[:, cols].bitcast(FP8X4),
-                        lhsT_scale=w_scales[:, cols],
-                        rhs=words[s][:].bitcast(FP8X4),
-                        rhs_scale=scales[s][:],
-                        start=(h == 0),
-                        stop=(h == 1),
-                    )
-                z = stage.tile([P, SLICE], F32, name="zd")
-                nc.vector.tensor_tensor(z[:], y[:], ts_g[s][:], ALU.mult)
-                if s == SLICES - 1 and m == M // P - 1:
-                    result = stage.tile([P, SLICE], F32, name="result")
-                    nc.vector.tensor_scalar(result[:], z[:], b_col[:, m : m + 1], None, ALU.add)
-                    nc.sync.dma_start(out[m * P : (m + 1) * P, s * SLICE : (s + 1) * SLICE], result[:])
-                else:
-                    finish(z, s, m)
-
-        gather_words(0)
+        gather_words(0, "words0")
+        project(0, 0)
+        project(0, 1)
+        evacuate(0, 0)
+        evacuate(0, 1)
+        gather_words(1, "words1")
+        project(1, 0)
+        project(1, 1)
+        evacuate(1, 0)
+        gather_words(2, "words2")
+        project(2, 0)
+        project(2, 1)
         gather_ts(0)
-        project_turned(0)
-        gather_words(1)
+        scale(nc.gpsimd, 0, 0)
         gather_ts(1)
-        project_turned(1)
-        gather_words(2)
+        scale(nc.gpsimd, 0, 1)
+        finish(False, 0, 0)
         gather_ts(2)
-        project_direct(2)
+        scale(nc.gpsimd, 1, 0)
+        finish(False, 0, 1)
+        scale(nc.vector, 1, 1)
+        finish(False, 1, 1)
+        scale(nc.vector, 2, 0)
+        scale(nc.vector, 2, 1)
+        finish(False, 1, 0)
+        finish(True, 2, 0)
+        finish(True, 2, 1)

@@ -21,7 +21,7 @@ SLICE = 512
 SLICES = S // SLICE
 TILES = SLICE // P
 HI_MASK = -(1 << 20)
-TS_TAIL = 2048
+TS_TAIL = 1024
 TS_HEAD = T - TS_TAIL
 RUN = TS_HEAD // P
 QUAD = 4
@@ -32,6 +32,7 @@ def tile_list_tabts_bias_kernel(tc, tab_words, tab_scales, w, ts, b, offs, out):
     with ExitStack() as ctx:
         keep = ctx.enter_context(tc.tile_pool(name="keep", bufs=1))
         windows = ctx.enter_context(tc.tile_pool(name="windows", bufs=1))
+        later = ctx.enter_context(tc.tile_pool(name="later", bufs=1))
         stage = ctx.enter_context(tc.tile_pool(name="stage", bufs=6))
         psum = ctx.enter_context(tc.psum_pool(name="psum", bufs=8))
 
@@ -73,7 +74,9 @@ def tile_list_tabts_bias_kernel(tc, tab_words, tab_scales, w, ts, b, offs, out):
 
         words = {}
         scales = [keep.tile([P, SLICE], U8, name="scales%d" % s, align_bytes=64) for s in range(SLICES)]
-        ts_g = [keep.tile([P, SLICE], F32, name="ts_g%d" % s, align_bytes=64) for s in range(SLICES)]
+        ts_g = {}
+        ones = later.tile([P, 4, SLICE], F32, name="ones", align_bytes=64, offset=0)
+        nc.vector.memset(ones[:, 0, :], 1.0)
 
         def list_slice(s):
             return offsets[:, s * (SLICE // 16) : (s + 1) * (SLICE // 16)]
@@ -81,12 +84,21 @@ def tile_list_tabts_bias_kernel(tc, tab_words, tab_scales, w, ts, b, offs, out):
         def gather_scales(s):
             nc.vector.tensor_copy(scales[s][:], scale_win[:].bitcast(U8).indirect(list_slice(s)))
 
-        def gather_words(s, tag):
-            words[s] = keep.tile([P, SLICE], U32, name="words%d" % s, tag=tag, align_bytes=64)
+        def gathered(s, place, dtype, name):
+            if s == 0:
+                return keep.tile([P, SLICE], dtype, name=name, align_bytes=64)
+            return later.tile([P, SLICE], dtype, name=name, align_bytes=64, offset=(2 * (s - 1) + place) * 4 * SLICE)
+
+        def gather_words(s):
+            words[s] = gathered(s, 0, U32, "words%d" % s)
             nc.vector.tensor_copy(words[s][:], word_win[:].bitcast(U32).indirect(list_slice(s)))
 
         def gather_ts(s):
-            nc.vector.tensor_copy(ts_g[s][:], ts_win[:].indirect(list_slice(s)))
+            ts_g[s] = gathered(s, 1, F32, "ts_g%d" % s)
+            if s == 0:
+                nc.vector.tensor_tensor(ts_g[s][:], ts_win[:].indirect(list_slice(s)), ones[:, 0, :], ALU.mult)
+            else:
+                nc.vector.tensor_copy(ts_g[s][:], ts_win[:].indirect(list_slice(s)))
 
         w_grouped = w_raw[:].rearrange("p t n -> p n t")
         w_hi = keep.tile([P, M, PACK], I32, name="w_hi", align_bytes=64)
@@ -98,6 +110,8 @@ def tile_list_tabts_bias_kernel(tc, tab_words, tab_scales, w, ts, b, offs, out):
             w_hi[:], w_raw[:].bitcast(I32).rearrange("p t n -> p n t"), HI_MASK, None, ALU.bitwise_and
         )
 
+        nc.scalar.activation(parts[:, 0, :, :], w_hi[:].bitcast(F32), ACT.Copy)
+
         ts_cells = ts_win[:, :TS_HEAD].rearrange("m (p c) -> m p c", c=RUN)
         for q in range(RUN // QUAD):
             spread = psum.tile([P, QUAD, P], F32, name="spread", tag="bank")
@@ -107,8 +121,6 @@ def tile_list_tabts_bias_kernel(tc, tab_words, tab_scales, w, ts, b, offs, out):
             nc.scalar.activation(
                 ts_cells[:, :, q * QUAD : (q + 1) * QUAD], spread[:].rearrange("m c p -> m p c"), ACT.Copy
             )
-            if q == 0:
-                nc.scalar.activation(parts[:, 0, :, :], w_hi[:].bitcast(F32), ACT.Copy)
 
         gather_scales(0)
         nc.gpsimd.tensor_tensor(parts[:, 1, :, :], w_grouped, w_hi[:].bitcast(F32), ALU.subtract)
@@ -147,37 +159,40 @@ def tile_list_tabts_bias_kernel(tc, tab_words, tab_scales, w, ts, b, offs, out):
             scaled[s, m] = z
 
         def finish(on_vector, s, m):
-            result = stage.tile([P, SLICE], F32, name="result")
+            if (s, m) == (0, 1):
+                result = later.tile([P, SLICE], F32, name="result01", align_bytes=64, offset=0)
+            else:
+                result = stage.tile([P, SLICE], F32, name="result")
             if on_vector:
                 nc.vector.tensor_scalar(result[:], scaled[s, m][:], b_col[:, m : m + 1], None, ALU.add)
             else:
                 nc.scalar.activation(result[:], scaled[s, m][:], ACT.Identity, bias=b_col[:, m : m + 1])
             nc.sync.dma_start(out[m * P : (m + 1) * P, s * SLICE : (s + 1) * SLICE], result[:])
 
-        gather_words(0, "words0")
+        gather_words(0)
         project(0, 0)
         project(0, 1)
+        gather_ts(0)
         evacuate(0, 0)
         evacuate(0, 1)
-        gather_words(1, "words1")
+        scale(nc.gpsimd, 0, 0)
+        gather_words(1)
         project(1, 0)
         project(1, 1)
+        gather_ts(1)
         evacuate(1, 0)
-        gather_words(2, "words2")
+        finish(False, 0, 0)
+        scale(nc.gpsimd, 0, 1)
+        scale(nc.vector, 1, 1)
+        gather_words(2)
         project(2, 0)
         project(2, 1)
-        gather_ts(0)
-        scale(nc.gpsimd, 0, 0)
-        gather_ts(1)
-        scale(nc.gpsimd, 0, 1)
-        finish(False, 0, 0)
         gather_ts(2)
-        scale(nc.gpsimd, 1, 0)
-        finish(False, 0, 1)
-        scale(nc.vector, 1, 1)
         finish(False, 1, 1)
+        finish(False, 0, 1)
+        scale(nc.gpsimd, 1, 0)
+        finish(False, 1, 0)
         scale(nc.vector, 2, 0)
         scale(nc.vector, 2, 1)
-        finish(False, 1, 0)
-        finish(True, 2, 0)
+        finish(False, 2, 0)
         finish(True, 2, 1)

@@ -1,6 +1,7 @@
 from contextlib import ExitStack
 
 import concourse.mybir as mybir
+from concourse.masks import make_identity
 
 K, M, T, S = 512, 256, 4096, 1536
 FLOPS = 2 * 2 * K * M * S
@@ -41,15 +42,15 @@ def tile_list_tabts_bias_kernel(tc, tab_words, tab_scales, w, ts, b, offs, out):
         ts_runs = keep.tile([P, RUN], F32, name="ts_runs")
         nc.sync.dma_start(ts_runs[:], ts[0, :TS_HEAD].rearrange("(p c) -> p c", c=RUN))
 
+        zero = windows.tile([P, 128], F32, name="zero", align_bytes=64, offset=4 * T - 256)
+        nc.vector.memset(zero[:, 0:1], 0.0)
         scale_win = keep.tile([P, T // 4], I32, name="scale_win", align_bytes=64)
         nc.vector.memset(scale_win[:], 0)
+        ones = later.tile([P, 4, SLICE], F32, name="ones", align_bytes=64, offset=0)
+        nc.vector.tensor_scalar(ones[:, 0, :], zero[:, 0:1].to_broadcast([P, SLICE]), 1.0, None, ALU.add)
 
-        zeros = windows.tile([P, P], F32, name="zeros", align_bytes=64, offset=4 * T - 256)
-        nc.vector.memset(zeros[:], 0.0)
         ident = keep.tile([P, P], F32, name="ident")
-        nc.gpsimd.affine_select(
-            out=ident[:], in_=zeros[:], pattern=[[-1, P]], compare_op=ALU.not_equal, fill=1.0, base=0, channel_multiplier=1
-        )
+        make_identity(nc, ident[:])
 
         w_raw = keep.tile([P, PACK, M], F32, name="w_raw", align_bytes=64)
         nc.sync.dma_start(w_raw[:], w.rearrange("(p t) n -> p t n", t=PACK))
@@ -73,10 +74,9 @@ def tile_list_tabts_bias_kernel(tc, tab_words, tab_scales, w, ts, b, offs, out):
             nc.sync.dma_start(b_col[:], b.rearrange("(m p) -> p m", p=P))
 
         words = {}
-        scales = [keep.tile([P, SLICE], U8, name="scales%d" % s, align_bytes=64) for s in range(SLICES)]
+        scales = [keep.tile([P, SLICE], U8, name="scales%d" % s, align_bytes=64) for s in (0, 2)]
+        scales = [scales[0], later.tile([P, SLICE], U8, name="scales1", align_bytes=64, offset=16 * SLICE), scales[1]]
         ts_g = {}
-        ones = later.tile([P, 4, SLICE], F32, name="ones", align_bytes=64, offset=0)
-        nc.vector.memset(ones[:, 0, :], 1.0)
 
         def list_slice(s):
             return offsets[:, s * (SLICE // 16) : (s + 1) * (SLICE // 16)]
@@ -87,7 +87,7 @@ def tile_list_tabts_bias_kernel(tc, tab_words, tab_scales, w, ts, b, offs, out):
         def gathered(s, place, dtype, name):
             if s == 0:
                 return keep.tile([P, SLICE], dtype, name=name, align_bytes=64)
-            return later.tile([P, SLICE], dtype, name=name, align_bytes=64, offset=(2 * (s - 1) + place) * 4 * SLICE)
+            return later.tile([P, SLICE], dtype, name=name, align_bytes=64, offset=(2 * (s - 1) + place) * 4 * SLICE + (SLICE if (s, place) == (2, 1) else 0))
 
         def gather_words(s):
             words[s] = gathered(s, 0, U32, "words%d" % s)
@@ -153,21 +153,22 @@ def tile_list_tabts_bias_kernel(tc, tab_words, tab_scales, w, ts, b, offs, out):
             nc.scalar.activation(y_out[:], sums[s, m][:], ACT.Copy)
             sums[s, m] = y_out
 
-        def scale(engine, s, m):
-            z = stage.tile([P, SLICE], F32, name="z")
-            engine.tensor_tensor(z[:], sums[s, m][:], ts_g[s][:], ALU.mult)
-            scaled[s, m] = z
+        def scale(engine, s, m, cols=slice(0, SLICE)):
+            z = stage.tile([P, cols.stop - cols.start], F32, name="z", bufs=8)
+            engine.tensor_tensor(z[:], sums[s, m][:, cols], ts_g[s][:, cols], ALU.mult)
+            scaled[s, m, cols.start] = z
 
-        def finish(on_vector, s, m):
+        def finish(on_vector, s, m, cols=slice(0, SLICE)):
             if (s, m) == (0, 1):
                 result = later.tile([P, SLICE], F32, name="result01", align_bytes=64, offset=0)
             else:
-                result = stage.tile([P, SLICE], F32, name="result")
+                result = stage.tile([P, cols.stop - cols.start], F32, name="result", bufs=8)
+            z = scaled[s, m, cols.start]
             if on_vector:
-                nc.vector.tensor_scalar(result[:], scaled[s, m][:], b_col[:, m : m + 1], None, ALU.add)
+                nc.vector.tensor_scalar(result[:], z[:], b_col[:, m : m + 1], None, ALU.add)
             else:
-                nc.scalar.activation(result[:], scaled[s, m][:], ACT.Identity, bias=b_col[:, m : m + 1])
-            nc.sync.dma_start(out[m * P : (m + 1) * P, s * SLICE : (s + 1) * SLICE], result[:])
+                nc.scalar.activation(result[:], z[:], ACT.Identity, bias=b_col[:, m : m + 1])
+            nc.sync.dma_start(out[m * P : (m + 1) * P, s * SLICE + cols.start : s * SLICE + cols.stop], result[:])
 
         gather_words(0)
         project(0, 0)
@@ -192,7 +193,11 @@ def tile_list_tabts_bias_kernel(tc, tab_words, tab_scales, w, ts, b, offs, out):
         finish(False, 0, 1)
         scale(nc.gpsimd, 1, 0)
         finish(False, 1, 0)
-        scale(nc.vector, 2, 0)
-        scale(nc.vector, 2, 1)
-        finish(False, 2, 0)
-        finish(True, 2, 1)
+        scale(nc.vector, 2, 0, slice(0, 256))
+        scale(nc.vector, 2, 1, slice(0, 256))
+        finish(False, 2, 0, slice(0, 256))
+        scale(nc.vector, 2, 0, slice(256, 512))
+        finish(False, 2, 1, slice(0, 256))
+        scale(nc.vector, 2, 1, slice(256, 512))
+        finish(False, 2, 0, slice(256, 512))
+        finish(True, 2, 1, slice(256, 512))

@@ -19,88 +19,55 @@ ACT = mybir.ActivationFunctionType
 P = 128
 PACK = 4
 SLICE = 512
-SLICES = S // SLICE
-TILES = SLICE // P
+HALF = SLICE // 2
 HI_MASK = -(1 << 20)
-TS_TAIL = 1024
+TS_TAIL = 512
 TS_HEAD = T - TS_TAIL
 RUN = TS_HEAD // P
 QUAD = 4
+CAST_AFTER = 2
+ROW = 4 * SLICE
+BEHIND = ROW
 
 
 def tile_list_tabts_bias_kernel(tc, tab_words, tab_scales, w, ts, b, offs, out):
     nc = tc.nc
     with ExitStack() as ctx:
         keep = ctx.enter_context(tc.tile_pool(name="keep", bufs=1))
-        windows = ctx.enter_context(tc.tile_pool(name="windows", bufs=1))
-        later = ctx.enter_context(tc.tile_pool(name="later", bufs=1))
-        stage = ctx.enter_context(tc.tile_pool(name="stage", bufs=6))
+        first_use = ctx.enter_context(tc.tile_pool(name="first_use", bufs=1))
+        late = ctx.enter_context(tc.tile_pool(name="late", bufs=1))
+        early = ctx.enter_context(tc.tile_pool(name="early", bufs=1))
+        stage = ctx.enter_context(tc.tile_pool(name="stage", bufs=8))
         psum = ctx.enter_context(tc.psum_pool(name="psum", bufs=8))
 
         offsets = keep.tile([P, S // 16], U16, name="offsets")
 
         ts_runs = keep.tile([P, RUN], F32, name="ts_runs")
         nc.sync.dma_start(ts_runs[:], ts[0, :TS_HEAD].rearrange("(p c) -> p c", c=RUN))
+        w_raw = keep.tile([P, PACK, M], F32, name="w_raw", align_bytes=64)
+        nc.sync.dma_start(w_raw[:], w.rearrange("(p t) n -> p t n", t=PACK))
+        nc.sync.dma_start(offsets[:], offs)
 
-        zero = windows.tile([P, 128], F32, name="zero", align_bytes=64, offset=4 * T - 256)
-        nc.vector.memset(zero[:, 0:1], 0.0)
-        scale_win = keep.tile([P, T // 4], I32, name="scale_win", align_bytes=64)
+        zero = early.tile([P, P], I32, name="zero", align_bytes=64, offset=4 * T - 256)
+        nc.vector.memset(zero[:, 0:1], 0)
+        scale_win = first_use.tile([P, T // 4], I32, name="scale_win", align_bytes=64, offset=0)
         nc.vector.memset(scale_win[:], 0)
-        ones = later.tile([P, 4, SLICE], F32, name="ones", align_bytes=64, offset=0)
-        nc.vector.tensor_scalar(ones[:, 0, :], zero[:, 0:1].to_broadcast([P, SLICE]), 1.0, None, ALU.add)
-
+        plane = keep.tile([P, S // 4], I32, name="plane", align_bytes=64)
+        nc.vector.tensor_copy(plane[:], zero[:, 0:1].to_broadcast([P, S // 4]))
         ident = keep.tile([P, P], F32, name="ident")
         make_identity(nc, ident[:])
 
-        w_raw = keep.tile([P, PACK, M], F32, name="w_raw", align_bytes=64)
-        nc.sync.dma_start(w_raw[:], w.rearrange("(p t) n -> p t n", t=PACK))
+        nc.sync.dma_start(scale_win[0:P:8, :], tab_scales[0].bitcast(I32))
 
-        nc.sync.dma_start(offsets[:], offs)
+        word_win = early.tile([P, T], I32, name="word_win", align_bytes=64, offset=0)
+        nc.sync.dma_start(word_win[:], tab_words[0].rearrange("p t i -> p (t i)").bitcast(I32))
 
-        scale_rows = tab_scales[0].bitcast(I32)
-        for r in range(4):
-            nc.sync.dma_start(scale_win[r:P:32, :], scale_rows[r:16:4, :])
-
-        word_win = windows.tile([P, T], I32, name="word_win", align_bytes=64, offset=0)
-        word_rows = tab_words[0].rearrange("p t i -> p (t i)").bitcast(I32)
-        for c0 in range(0, T, T // 1):
-            nc.sync.dma_start(word_win[:, c0 : c0 + T // 1], word_rows[:, c0 : c0 + T // 1])
-
-        ts_win = windows.tile([P, T], F32, name="ts_win", align_bytes=64, offset=4 * T + 64)
+        ts_win = early.tile([P, T], F32, name="ts_win", align_bytes=64, offset=4 * T)
         nc.sync.dma_start(ts_win[:, TS_HEAD:], ts[:, TS_HEAD:])
-
-        b_col = windows.tile([P, M // P], F32, name="b_col", align_bytes=64, offset=4 * T)
-        with nc.allow_non_contiguous_dma(reason="one bias value to a partition"):
-            nc.sync.dma_start(b_col[:], b.rearrange("(m p) -> p m", p=P))
-
-        words = {}
-        scales = [keep.tile([P, SLICE], U8, name="scales%d" % s, align_bytes=64) for s in (0, 2)]
-        scales = [scales[0], later.tile([P, SLICE], U8, name="scales1", align_bytes=64, offset=16 * SLICE), scales[1]]
-        ts_g = {}
 
         def list_slice(s):
             return offsets[:, s * (SLICE // 16) : (s + 1) * (SLICE // 16)]
 
-        def gather_scales(s):
-            nc.vector.tensor_copy(scales[s][:], scale_win[:].bitcast(U8).indirect(list_slice(s)))
-
-        def gathered(s, place, dtype, name):
-            if s == 0:
-                return keep.tile([P, SLICE], dtype, name=name, align_bytes=64)
-            return later.tile([P, SLICE], dtype, name=name, align_bytes=64, offset=(2 * (s - 1) + place) * 4 * SLICE + (SLICE if (s, place) == (2, 1) else 0))
-
-        def gather_words(s):
-            words[s] = gathered(s, 0, U32, "words%d" % s)
-            nc.vector.tensor_copy(words[s][:], word_win[:].bitcast(U32).indirect(list_slice(s)))
-
-        def gather_ts(s):
-            ts_g[s] = gathered(s, 1, F32, "ts_g%d" % s)
-            if s == 0:
-                nc.vector.tensor_tensor(ts_g[s][:], ts_win[:].indirect(list_slice(s)), ones[:, 0, :], ALU.mult)
-            else:
-                nc.vector.tensor_copy(ts_g[s][:], ts_win[:].indirect(list_slice(s)))
-
-        w_grouped = w_raw[:].rearrange("p t n -> p n t")
         w_hi = keep.tile([P, M, PACK], I32, name="w_hi", align_bytes=64)
         parts = keep.tile([P, 2, M, PACK], BF16, name="parts", align_bytes=64)
         w_codes = keep.tile([P, 2 * M], U32, name="w_codes", align_bytes=64)
@@ -109,8 +76,9 @@ def tile_list_tabts_bias_kernel(tc, tab_words, tab_scales, w, ts, b, offs, out):
         nc.vector.tensor_scalar(
             w_hi[:], w_raw[:].bitcast(I32).rearrange("p t n -> p n t"), HI_MASK, None, ALU.bitwise_and
         )
-
-        nc.scalar.activation(parts[:, 0, :, :], w_hi[:].bitcast(F32), ACT.Copy)
+        nc.gpsimd.tensor_tensor(
+            parts[:, 1, :, :], w_raw[:].rearrange("p t n -> p n t"), w_hi[:].bitcast(F32), ALU.subtract
+        )
 
         ts_cells = ts_win[:, :TS_HEAD].rearrange("m (p c) -> m p c", c=RUN)
         for q in range(RUN // QUAD):
@@ -121,83 +89,107 @@ def tile_list_tabts_bias_kernel(tc, tab_words, tab_scales, w, ts, b, offs, out):
             nc.scalar.activation(
                 ts_cells[:, :, q * QUAD : (q + 1) * QUAD], spread[:].rearrange("m c p -> m p c"), ACT.Copy
             )
+            if q == CAST_AFTER:
+                nc.scalar.activation(parts[:, 0, :, :], w_hi[:].bitcast(F32), ACT.Copy)
 
-        gather_scales(0)
-        nc.gpsimd.tensor_tensor(parts[:, 1, :, :], w_grouped, w_hi[:].bitcast(F32), ALU.subtract)
-        gather_scales(1)
-        nc.vector.quantize_mx(
-            out=w_codes[:].bitcast(FP8X4), scales=w_scales[:], in_=parts[:].rearrange("p h n t -> p (h n t)")
-        )
-        gather_scales(2)
+        picked = late.tile([P, S], U8, name="picked", align_bytes=64, offset=BEHIND - SLICE)
+        nc.vector.tensor_copy(picked[:], scale_win[:].bitcast(U8).indirect(offsets[:]))
+        for r in range(4):
+            nc.sync.dma_start(plane[r:P:32, :], picked[8 * r : P : 32, :].bitcast(I32))
+        scales = [plane[:].bitcast(U8)[:, s * SLICE : (s + 1) * SLICE] for s in range(3)]
+
+        b_col = first_use.tile([P, M // P], F32, name="b_col", align_bytes=64, offset=0)
+        with nc.allow_non_contiguous_dma(reason="one bias value to a partition"):
+            nc.sync.dma_start(b_col[:], b.rearrange("(m p) -> p m", p=P))
+
+        ts_g = [
+            keep.tile([P, SLICE], F32, name="ts_g0", align_bytes=64),
+            late.tile([P, SLICE], F32, name="ts_g1", align_bytes=64, offset=BEHIND - ROW),
+        ]
+        words = [
+            keep.tile([P, SLICE], U32, name="words_even", align_bytes=64),
+            late.tile([P, SLICE], U32, name="words1", align_bytes=64, offset=BEHIND),
+        ]
+
+        def gather_words(s):
+            if s == 2:
+                words.append(keep.tile([P, SLICE], U32, name="words_even", align_bytes=64))
+            nc.vector.tensor_copy(words[s][:], word_win[:].bitcast(U32).indirect(list_slice(s)))
+
+        def gather_ts(s):
+            nc.vector.tensor_copy(ts_g[s][:], ts_win[:].indirect(list_slice(s)))
 
         sums = {}
         scaled = {}
 
-        def project(s, m):
-            y = psum.tile([P, SLICE], F32, name="y", tag="bank")
+        def project(s, m, tokens):
+            y = psum.tile([P, tokens.stop - tokens.start], F32, name="y", tag="bank")
             for h in range(2):
                 cols = slice(h * M + m * P, h * M + (m + 1) * P)
                 nc.tensor.matmul_mx(
                     out=y[:],
                     lhsT=w_codes[:, cols].bitcast(FP8X4),
                     lhsT_scale=w_scales[:, cols],
-                    rhs=words[s][:].bitcast(FP8X4),
-                    rhs_scale=scales[s][:],
+                    rhs=words[s][:, tokens].bitcast(FP8X4),
+                    rhs_scale=scales[s][:, tokens],
                     start=(h == 0),
                     stop=(h == 1),
                 )
-            sums[s, m] = y
+            sums[s, m, tokens.start] = y
 
-        def evacuate(s, m):
-            y_out = keep.tile([P, SLICE], F32, name="y_out", tag="y_out%d%d" % (s, m), align_bytes=64)
-            nc.scalar.activation(y_out[:], sums[s, m][:], ACT.Copy)
-            sums[s, m] = y_out
+        def scale_on_gpsimd(s, m, pieces, place):
+            y_out = late.tile([P, SLICE], F32, name="y_out%d%d" % (s, m), align_bytes=64, offset=BEHIND + place * ROW)
+            z = stage.tile([P, SLICE], F32, name="z")
+            for tokens in pieces:
+                nc.scalar.activation(y_out[:, tokens], sums[s, m, tokens.start][:], ACT.Copy)
+                nc.gpsimd.tensor_tensor(z[:, tokens], y_out[:, tokens], ts_g[s][:, tokens], ALU.mult)
+            scaled[s, m] = z[:]
 
-        def scale(engine, s, m, cols=slice(0, SLICE)):
-            z = stage.tile([P, cols.stop - cols.start], F32, name="z", bufs=8)
-            engine.tensor_tensor(z[:], sums[s, m][:, cols], ts_g[s][:, cols], ALU.mult)
-            scaled[s, m, cols.start] = z
+        def scale_on_vector(z, s, m, tokens):
+            scaled[s, m] = z
+            nc.vector.tensor_tensor(z[:, tokens], sums[s, m, 0][:, tokens], ts_g[s][:, tokens], ALU.mult)
 
-        def finish(on_vector, s, m, cols=slice(0, SLICE)):
-            if (s, m) == (0, 1):
-                result = later.tile([P, SLICE], F32, name="result01", align_bytes=64, offset=0)
-            else:
-                result = stage.tile([P, cols.stop - cols.start], F32, name="result", bufs=8)
-            z = scaled[s, m, cols.start]
+        def finish(on_vector, s, m, tokens):
+            result = stage.tile([P, tokens.stop - tokens.start], F32, name="result")
+            z = scaled[s, m][:, tokens]
             if on_vector:
-                nc.vector.tensor_scalar(result[:], z[:], b_col[:, m : m + 1], None, ALU.add)
+                nc.vector.tensor_scalar(result[:], z, b_col[:, m : m + 1], None, ALU.add)
             else:
-                nc.scalar.activation(result[:], z[:], ACT.Identity, bias=b_col[:, m : m + 1])
-            nc.sync.dma_start(out[m * P : (m + 1) * P, s * SLICE + cols.start : s * SLICE + cols.stop], result[:])
+                nc.scalar.activation(result[:], z, ACT.Identity, bias=b_col[:, m : m + 1])
+            nc.sync.dma_start(out[m * P : (m + 1) * P, s * SLICE + tokens.start : s * SLICE + tokens.stop], result[:])
 
+        whole, first, second = slice(0, SLICE), slice(0, HALF), slice(HALF, SLICE)
+
+        nc.vector.quantize_mx(
+            out=w_codes[:].bitcast(FP8X4), scales=w_scales[:], in_=parts[:].rearrange("p h n t -> p (h n t)")
+        )
         gather_words(0)
-        project(0, 0)
-        project(0, 1)
+        project(0, 0, first)
+        project(0, 0, second)
+        project(0, 1, whole)
         gather_ts(0)
-        evacuate(0, 0)
-        evacuate(0, 1)
-        scale(nc.gpsimd, 0, 0)
-        gather_words(1)
-        project(1, 0)
-        project(1, 1)
-        gather_ts(1)
-        evacuate(1, 0)
-        finish(False, 0, 0)
-        scale(nc.gpsimd, 0, 1)
-        scale(nc.vector, 1, 1)
-        gather_words(2)
-        project(2, 0)
-        project(2, 1)
+        for s in (1, 2):
+            gather_words(s)
+            project(s, 0, whole)
+            project(s, 1, whole)
+            if s == 1:
+                gather_ts(s)
+
+        scale_on_gpsimd(0, 0, (first, second), 1)
+        scale_on_gpsimd(0, 1, (whole,), 3)
+        scale_on_gpsimd(1, 0, (whole,), 4)
+        finish(False, 0, 0, whole)
+        finish(False, 0, 1, whole)
+
+        ts_g.append(late.tile([P, SLICE], F32, name="ts_g2", align_bytes=64, offset=BEHIND + ROW // 2))
+        z_mid = late.tile([P, SLICE], F32, name="z_mid", align_bytes=64, offset=BEHIND + 3 * ROW // 2)
+        z_last = late.tile([P, 2, SLICE], F32, name="z_last", align_bytes=64, offset=BEHIND + 4 * ROW)
+
+        scale_on_vector(z_mid[:], 1, 1, whole)
         gather_ts(2)
-        finish(False, 1, 1)
-        finish(False, 0, 1)
-        scale(nc.gpsimd, 1, 0)
-        finish(False, 1, 0)
-        scale(nc.vector, 2, 0, slice(0, 256))
-        scale(nc.vector, 2, 1, slice(0, 256))
-        finish(False, 2, 0, slice(0, 256))
-        scale(nc.vector, 2, 0, slice(256, 512))
-        finish(False, 2, 1, slice(0, 256))
-        scale(nc.vector, 2, 1, slice(256, 512))
-        finish(False, 2, 0, slice(256, 512))
-        finish(True, 2, 1, slice(256, 512))
+        finish(False, 1, 1, whole)
+        finish(False, 1, 0, whole)
+        for m in range(2):
+            for tokens in (first, second):
+                scale_on_vector(z_last[:, m, :], 2, m, tokens)
+                finish((m, tokens) == (1, second), 2, m, tokens)

@@ -34,10 +34,9 @@ def tile_list_tabts_bias_kernel(tc, tab_words, tab_scales, w, ts, b, offs, out):
     nc = tc.nc
     with ExitStack() as ctx:
         keep = ctx.enter_context(tc.tile_pool(name="keep", bufs=1))
-        first_use = ctx.enter_context(tc.tile_pool(name="first_use", bufs=1))
         late = ctx.enter_context(tc.tile_pool(name="late", bufs=1))
         early = ctx.enter_context(tc.tile_pool(name="early", bufs=1))
-        stage = ctx.enter_context(tc.tile_pool(name="stage", bufs=8))
+        stage = ctx.enter_context(tc.tile_pool(name="stage", bufs=10))
         psum = ctx.enter_context(tc.psum_pool(name="psum", bufs=8))
 
         offsets = keep.tile([P, S // 16], U16, name="offsets")
@@ -50,7 +49,7 @@ def tile_list_tabts_bias_kernel(tc, tab_words, tab_scales, w, ts, b, offs, out):
 
         zero = early.tile([P, P], I32, name="zero", align_bytes=64, offset=4 * T - 256)
         nc.vector.memset(zero[:, 0:1], 0)
-        scale_win = first_use.tile([P, T // 4], I32, name="scale_win", align_bytes=64, offset=0)
+        scale_win = keep.tile([P, T // 4], I32, name="scale_win", align_bytes=64)
         nc.vector.memset(scale_win[:], 0)
         plane = keep.tile([P, S // 4], I32, name="plane", align_bytes=64)
         nc.vector.tensor_copy(plane[:], zero[:, 0:1].to_broadcast([P, S // 4]))
@@ -62,8 +61,12 @@ def tile_list_tabts_bias_kernel(tc, tab_words, tab_scales, w, ts, b, offs, out):
         word_win = early.tile([P, T], I32, name="word_win", align_bytes=64, offset=0)
         nc.sync.dma_start(word_win[:], tab_words[0].rearrange("p t i -> p (t i)").bitcast(I32))
 
-        ts_win = early.tile([P, T], F32, name="ts_win", align_bytes=64, offset=4 * T)
+        ts_win = early.tile([P, T], F32, name="ts_win", align_bytes=64, offset=4 * T + 64)
         nc.sync.dma_start(ts_win[:, TS_HEAD:], ts[:, TS_HEAD:])
+
+        b_col = early.tile([P, M // P], F32, name="b_col", align_bytes=64, offset=4 * T)
+        with nc.allow_non_contiguous_dma(reason="one bias value to a partition"):
+            nc.sync.dma_start(b_col[:], b.rearrange("(m p) -> p m", p=P))
 
         def list_slice(s):
             return offsets[:, s * (SLICE // 16) : (s + 1) * (SLICE // 16)]
@@ -97,10 +100,6 @@ def tile_list_tabts_bias_kernel(tc, tab_words, tab_scales, w, ts, b, offs, out):
         for r in range(4):
             nc.sync.dma_start(plane[r:P:32, :], picked[8 * r : P : 32, :].bitcast(I32))
         scales = [plane[:].bitcast(U8)[:, s * SLICE : (s + 1) * SLICE] for s in range(3)]
-
-        b_col = first_use.tile([P, M // P], F32, name="b_col", align_bytes=64, offset=0)
-        with nc.allow_non_contiguous_dma(reason="one bias value to a partition"):
-            nc.sync.dma_start(b_col[:], b.rearrange("(m p) -> p m", p=P))
 
         ts_g = [
             keep.tile([P, SLICE], F32, name="ts_g0", align_bytes=64),
@@ -137,12 +136,21 @@ def tile_list_tabts_bias_kernel(tc, tab_words, tab_scales, w, ts, b, offs, out):
                 )
             sums[s, m, tokens.start] = y
 
-        def scale_on_gpsimd(s, m, pieces, place):
+        def scale_on_gpsimd(s, m, products, place):
             y_out = late.tile([P, SLICE], F32, name="y_out%d%d" % (s, m), align_bytes=64, offset=BEHIND + place * ROW)
             z = stage.tile([P, SLICE], F32, name="z")
-            for tokens in pieces:
+            for tokens in (first, second):
                 nc.scalar.activation(y_out[:, tokens], sums[s, m, tokens.start][:], ACT.Copy)
+            for tokens in products:
                 nc.gpsimd.tensor_tensor(z[:, tokens], y_out[:, tokens], ts_g[s][:, tokens], ALU.mult)
+            scaled[s, m] = z[:]
+
+        def scale_halves_on_gpsimd(s, m, places):
+            z = stage.tile([P, SLICE], F32, name="z")
+            for tokens, place in zip((first, second), places):
+                y_half = late.tile([P, HALF], F32, name="y_half%d" % place, align_bytes=64, offset=BEHIND + place * ROW)
+                nc.scalar.activation(y_half[:], sums[s, m, 0][:, tokens], ACT.Copy)
+                nc.gpsimd.tensor_tensor(z[:, tokens], y_half[:], ts_g[s][:, tokens], ALU.mult)
             scaled[s, m] = z[:]
 
         def scale_on_vector(z, s, m, tokens):
@@ -166,7 +174,8 @@ def tile_list_tabts_bias_kernel(tc, tab_words, tab_scales, w, ts, b, offs, out):
         gather_words(0)
         project(0, 0, first)
         project(0, 0, second)
-        project(0, 1, whole)
+        project(0, 1, first)
+        project(0, 1, second)
         gather_ts(0)
         for s in (1, 2):
             gather_words(s)
@@ -177,7 +186,7 @@ def tile_list_tabts_bias_kernel(tc, tab_words, tab_scales, w, ts, b, offs, out):
 
         scale_on_gpsimd(0, 0, (first, second), 1)
         scale_on_gpsimd(0, 1, (whole,), 3)
-        scale_on_gpsimd(1, 0, (whole,), 4)
+        scale_halves_on_gpsimd(1, 0, (4, 6))
         finish(False, 0, 0, whole)
         finish(False, 0, 1, whole)
 
@@ -185,11 +194,20 @@ def tile_list_tabts_bias_kernel(tc, tab_words, tab_scales, w, ts, b, offs, out):
         z_mid = late.tile([P, SLICE], F32, name="z_mid", align_bytes=64, offset=BEHIND + 3 * ROW // 2)
         z_last = late.tile([P, 2, SLICE], F32, name="z_last", align_bytes=64, offset=BEHIND + 4 * ROW)
 
-        scale_on_vector(z_mid[:], 1, 1, whole)
+        scale_on_vector(z_mid[:], 1, 1, first)
         gather_ts(2)
-        finish(False, 1, 1, whole)
-        finish(False, 1, 0, whole)
-        for m in range(2):
-            for tokens in (first, second):
-                scale_on_vector(z_last[:, m, :], 2, m, tokens)
-                finish((m, tokens) == (1, second), 2, m, tokens)
+        finish(False, 1, 1, first)
+        y_last = late.tile([P, HALF], F32, name="y_last", align_bytes=64, offset=BEHIND + 7 * ROW)
+        nc.scalar.activation(y_last[:], sums[1, 1, 0][:, second], ACT.Copy)
+        nc.gpsimd.tensor_tensor(z_mid[:, second], y_last[:], ts_g[1][:, second], ALU.mult)
+        finish(False, 1, 0, first)
+        finish(False, 1, 0, second)
+        scale_on_vector(z_last[:, 0, :], 2, 0, first)
+        finish(False, 2, 0, first)
+        scale_on_vector(z_last[:, 0, :], 2, 0, second)
+        finish(False, 1, 1, second)
+        finish(False, 2, 0, second)
+        for tokens in (first, second):
+            scale_on_vector(z_last[:, 1, :], 2, 1, tokens)
+        for tokens in (first, second):
+            finish(True, 2, 1, tokens)

@@ -41,10 +41,10 @@ def tile_list_tabts_bias_kernel(tc, tab_words, tab_scales, w, ts, b, offs, out):
 
         offsets = keep.tile([P, S // 16], U16, name="offsets")
 
-        ts_runs = keep.tile([P, RUN], F32, name="ts_runs")
-        nc.sync.dma_start(ts_runs[:], ts[0, :TS_HEAD].rearrange("(p c) -> p c", c=RUN))
         w_raw = keep.tile([P, PACK, M], F32, name="w_raw", align_bytes=64)
         nc.sync.dma_start(w_raw[:], w.rearrange("(p t) n -> p t n", t=PACK))
+        ts_runs = keep.tile([P, RUN], F32, name="ts_runs")
+        nc.sync.dma_start(ts_runs[:], ts[0, :TS_HEAD].rearrange("(p c) -> p c", c=RUN))
         nc.sync.dma_start(offsets[:], offs)
 
         zero = early.tile([P, P], I32, name="zero", align_bytes=64, offset=4 * T - 256)
@@ -157,13 +157,15 @@ def tile_list_tabts_bias_kernel(tc, tab_words, tab_scales, w, ts, b, offs, out):
             scaled[s, m] = z
             nc.vector.tensor_tensor(z[:, tokens], sums[s, m, 0][:, tokens], ts_g[s][:, tokens], ALU.mult)
 
-        def finish(on_vector, s, m, tokens):
+        def finish(engine, s, m, tokens):
             result = stage.tile([P, tokens.stop - tokens.start], F32, name="result")
             z = scaled[s, m][:, tokens]
-            if on_vector:
+            if engine == "scalar":
+                nc.scalar.activation(result[:], z, ACT.Identity, bias=b_col[:, m : m + 1])
+            elif engine == "vector":
                 nc.vector.tensor_scalar(result[:], z, b_col[:, m : m + 1], None, ALU.add)
             else:
-                nc.scalar.activation(result[:], z, ACT.Identity, bias=b_col[:, m : m + 1])
+                nc.gpsimd.tensor_scalar(result[:], z, 1.0, b_col[:, m : m + 1], ALU.mult, ALU.add)
             nc.sync.dma_start(out[m * P : (m + 1) * P, s * SLICE + tokens.start : s * SLICE + tokens.stop], result[:])
 
         whole, first, second = slice(0, SLICE), slice(0, HALF), slice(HALF, SLICE)
@@ -187,8 +189,8 @@ def tile_list_tabts_bias_kernel(tc, tab_words, tab_scales, w, ts, b, offs, out):
         scale_on_gpsimd(0, 0, (first, second), 1)
         scale_on_gpsimd(0, 1, (whole,), 3)
         scale_halves_on_gpsimd(1, 0, (4, 6))
-        finish(False, 0, 0, whole)
-        finish(False, 0, 1, whole)
+        finish("scalar", 0, 0, whole)
+        finish("scalar", 0, 1, whole)
 
         ts_g.append(late.tile([P, SLICE], F32, name="ts_g2", align_bytes=64, offset=BEHIND + ROW // 2))
         z_mid = late.tile([P, SLICE], F32, name="z_mid", align_bytes=64, offset=BEHIND + 3 * ROW // 2)
@@ -196,18 +198,18 @@ def tile_list_tabts_bias_kernel(tc, tab_words, tab_scales, w, ts, b, offs, out):
 
         scale_on_vector(z_mid[:], 1, 1, first)
         gather_ts(2)
-        finish(False, 1, 1, first)
+        finish("scalar", 1, 1, first)
         y_last = late.tile([P, HALF], F32, name="y_last", align_bytes=64, offset=BEHIND + 7 * ROW)
         nc.scalar.activation(y_last[:], sums[1, 1, 0][:, second], ACT.Copy)
         nc.gpsimd.tensor_tensor(z_mid[:, second], y_last[:], ts_g[1][:, second], ALU.mult)
-        finish(False, 1, 0, first)
-        finish(False, 1, 0, second)
+        finish("scalar", 1, 0, first)
+        finish("scalar", 1, 0, second)
         scale_on_vector(z_last[:, 0, :], 2, 0, first)
-        finish(False, 2, 0, first)
+        finish("scalar", 2, 0, first)
         scale_on_vector(z_last[:, 0, :], 2, 0, second)
-        finish(False, 1, 1, second)
-        finish(False, 2, 0, second)
+        finish("gpsimd", 1, 1, second)
+        finish("scalar", 2, 0, second)
         for tokens in (first, second):
             scale_on_vector(z_last[:, 1, :], 2, 1, tokens)
         for tokens in (first, second):
-            finish(True, 2, 1, tokens)
+            finish("vector", 2, 1, tokens)

@@ -196,20 +196,15 @@ def tile_list_tabts_bias_kernel(tc, tab_words, tab_scales, w, ts, b, offs, out):
         z_mid = late.tile([P, SLICE], F32, name="z_mid", align_bytes=64, offset=BEHIND + 3 * ROW // 2)
         z_last = late.tile([P, 2, SLICE], F32, name="z_last", align_bytes=64, offset=BEHIND + 4 * ROW)
 
-        scale_on_vector(z_mid[:], 1, 1, first)
+        scale_on_vector(z_mid[:], 1, 1, whole)
         gather_ts(2)
-        finish("scalar", 1, 1, first)
-        y_last = late.tile([P, HALF], F32, name="y_last", align_bytes=64, offset=BEHIND + 7 * ROW)
-        nc.scalar.activation(y_last[:], sums[1, 1, 0][:, second], ACT.Copy)
-        nc.gpsimd.tensor_tensor(z_mid[:, second], y_last[:], ts_g[1][:, second], ALU.mult)
+        finish("scalar", 1, 1, whole)
         finish("scalar", 1, 0, first)
-        finish("scalar", 1, 0, second)
-        scale_on_vector(z_last[:, 0, :], 2, 0, first)
-        finish("scalar", 2, 0, first)
-        scale_on_vector(z_last[:, 0, :], 2, 0, second)
-        finish("gpsimd", 1, 1, second)
-        finish("scalar", 2, 0, second)
+        finish("gpsimd", 1, 0, second)
         for tokens in (first, second):
-            scale_on_vector(z_last[:, 1, :], 2, 1, tokens)
-        for tokens in (first, second):
-            finish("vector", 2, 1, tokens)
+            scale_on_vector(z_last[:, 0, :], 2, 0, tokens)
+            finish("scalar", 2, 0, tokens)
+        scale_on_vector(z_last[:, 1, :], 2, 1, first)
+        finish("scalar", 2, 1, first)
+        scale_on_vector(z_last[:, 1, :], 2, 1, second)
+        finish("vector", 2, 1, second)

@@ -52,7 +52,8 @@ def tile_list_tabts_bias_kernel(tc, tab_words, tab_scales, w, ts, b, offs, out):
         scale_win = keep.tile([P, T // 4], I32, name="scale_win", align_bytes=64)
         nc.vector.memset(scale_win[:], 0)
         plane = keep.tile([P, S // 4], I32, name="plane", align_bytes=64)
-        nc.vector.tensor_copy(plane[:], zero[:, 0:1].to_broadcast([P, S // 4]))
+        nc.vector.tensor_copy(plane[:, :16], zero[:, 0:1].to_broadcast([P, 16]))
+        nc.vector.memset(plane[:, 16:], 0)
         ident = keep.tile([P, P], F32, name="ident")
         make_identity(nc, ident[:])
 
@@ -77,7 +78,11 @@ def tile_list_tabts_bias_kernel(tc, tab_words, tab_scales, w, ts, b, offs, out):
         w_scales = keep.tile([P, 2 * M], U8, name="w_scales", align_bytes=64)
 
         nc.vector.tensor_scalar(
-            w_hi[:], w_raw[:].bitcast(I32).rearrange("p t n -> p n t"), HI_MASK, None, ALU.bitwise_and
+            w_hi[:].rearrange("p (c i) t -> p c t i", i=4),
+            w_raw[:].bitcast(I32).rearrange("p t (c i) -> p c t i", i=4),
+            HI_MASK,
+            None,
+            ALU.bitwise_and,
         )
         nc.gpsimd.tensor_tensor(
             parts[:, 1, :, :], w_raw[:].rearrange("p t n -> p n t"), w_hi[:].bitcast(F32), ALU.subtract

@@ -28,6 +28,11 @@ QUAD = 4
 CAST_AFTER = 2
 ROW = 4 * SLICE
 BEHIND = ROW
+WORD_BYTES = 4 * T
+BIAS_BYTES = 64
+ZERO_COLUMNS = 16
+STAGES = 10
+BANKS = 8
 
 
 def tile_list_tabts_bias_kernel(tc, tab_words, tab_scales, w, ts, b, offs, out):
@@ -36,8 +41,8 @@ def tile_list_tabts_bias_kernel(tc, tab_words, tab_scales, w, ts, b, offs, out):
         keep = ctx.enter_context(tc.tile_pool(name="keep", bufs=1))
         late = ctx.enter_context(tc.tile_pool(name="late", bufs=1))
         early = ctx.enter_context(tc.tile_pool(name="early", bufs=1))
-        stage = ctx.enter_context(tc.tile_pool(name="stage", bufs=10))
-        psum = ctx.enter_context(tc.psum_pool(name="psum", bufs=8))
+        stage = ctx.enter_context(tc.tile_pool(name="stage", bufs=STAGES))
+        psum = ctx.enter_context(tc.psum_pool(name="psum", bufs=BANKS))
 
         offsets = keep.tile([P, S // 16], U16, name="offsets")
 
@@ -47,25 +52,25 @@ def tile_list_tabts_bias_kernel(tc, tab_words, tab_scales, w, ts, b, offs, out):
         nc.sync.dma_start(ts_runs[:], ts[0, :TS_HEAD].rearrange("(p c) -> p c", c=RUN))
         nc.sync.dma_start(offsets[:], offs)
 
-        zero = early.tile([P, P], I32, name="zero", align_bytes=64, offset=4 * T - 256)
+        zero = early.tile([P, P], I32, name="zero", align_bytes=64, offset=WORD_BYTES - 2 * P)
         nc.vector.memset(zero[:, 0:1], 0)
         scale_win = keep.tile([P, T // 4], I32, name="scale_win", align_bytes=64)
         nc.vector.memset(scale_win[:], 0)
         plane = keep.tile([P, S // 4], I32, name="plane", align_bytes=64)
-        nc.vector.tensor_copy(plane[:, :16], zero[:, 0:1].to_broadcast([P, 16]))
-        nc.vector.memset(plane[:, 16:], 0)
+        nc.vector.tensor_copy(plane[:, :ZERO_COLUMNS], zero[:, 0:1].to_broadcast([P, ZERO_COLUMNS]))
+        nc.vector.memset(plane[:, ZERO_COLUMNS:], 0)
         ident = keep.tile([P, P], F32, name="ident")
         make_identity(nc, ident[:])
 
-        nc.sync.dma_start(scale_win[0:P:8, :], tab_scales[0].bitcast(I32))
+        nc.sync.dma_start(scale_win[32:96:4, :], tab_scales[0].bitcast(I32))
 
         word_win = early.tile([P, T], I32, name="word_win", align_bytes=64, offset=0)
         nc.sync.dma_start(word_win[:], tab_words[0].rearrange("p t i -> p (t i)").bitcast(I32))
 
-        ts_win = early.tile([P, T], F32, name="ts_win", align_bytes=64, offset=4 * T + 64)
+        ts_win = early.tile([P, T], F32, name="ts_win", align_bytes=64, offset=WORD_BYTES + BIAS_BYTES)
         nc.sync.dma_start(ts_win[:, TS_HEAD:], ts[:, TS_HEAD:])
 
-        b_col = early.tile([P, M // P], F32, name="b_col", align_bytes=64, offset=4 * T)
+        b_col = early.tile([P, M // P], F32, name="b_col", align_bytes=64, offset=WORD_BYTES)
         with nc.allow_non_contiguous_dma(reason="one bias value to a partition"):
             nc.sync.dma_start(b_col[:], b.rearrange("(m p) -> p m", p=P))
 
@@ -103,7 +108,7 @@ def tile_list_tabts_bias_kernel(tc, tab_words, tab_scales, w, ts, b, offs, out):
         picked = late.tile([P, S], U8, name="picked", align_bytes=64, offset=BEHIND - SLICE)
         nc.vector.tensor_copy(picked[:], scale_win[:].bitcast(U8).indirect(offsets[:]))
         for r in range(4):
-            nc.sync.dma_start(plane[r:P:32, :], picked[8 * r : P : 32, :].bitcast(I32))
+            nc.sync.dma_start(plane[r:P:32, :], picked[32 + 4 * r : 96 : 16, :].bitcast(I32))
         scales = [plane[:].bitcast(U8)[:, s * SLICE : (s + 1) * SLICE] for s in range(3)]
 
         ts_g = [

@@ -18,8 +18,8 @@ ACT = mybir.ActivationFunctionType
 
 P = 128
 PACK = 4
-SLICE = 512
-HALF = SLICE // 2
+SLICE = 256
+SCALE_HEAD = 512
 HI_MASK = -(1 << 20)
 TS_TAIL = 512
 TS_HEAD = T - TS_TAIL
@@ -27,11 +27,11 @@ RUN = TS_HEAD // P
 QUAD = 4
 CAST_AFTER = 2
 ROW = 4 * SLICE
-BEHIND = ROW
+STEP = ROW - 64
 WORD_BYTES = 4 * T
 BIAS_BYTES = 64
 ZERO_COLUMNS = 16
-STAGES = 10
+STAGES = 6
 BANKS = 8
 
 
@@ -41,6 +41,8 @@ def tile_list_tabts_bias_kernel(tc, tab_words, tab_scales, w, ts, b, offs, out):
         keep = ctx.enter_context(tc.tile_pool(name="keep", bufs=1))
         late = ctx.enter_context(tc.tile_pool(name="late", bufs=1))
         early = ctx.enter_context(tc.tile_pool(name="early", bufs=1))
+        later = ctx.enter_context(tc.tile_pool(name="later", bufs=1))
+        ring = ctx.enter_context(tc.tile_pool(name="ring", bufs=1))
         stage = ctx.enter_context(tc.tile_pool(name="stage", bufs=STAGES))
         psum = ctx.enter_context(tc.psum_pool(name="psum", bufs=BANKS))
 
@@ -105,116 +107,156 @@ def tile_list_tabts_bias_kernel(tc, tab_words, tab_scales, w, ts, b, offs, out):
             if q == CAST_AFTER:
                 nc.scalar.activation(parts[:, 0, :, :], w_hi[:].bitcast(F32), ACT.Copy)
 
-        picked = late.tile([P, S], U8, name="picked", align_bytes=64, offset=BEHIND - SLICE)
-        nc.vector.tensor_copy(picked[:], scale_win[:].bitcast(U8).indirect(offsets[:]))
-        for r in range(4):
-            nc.sync.dma_start(plane[r:P:32, :], picked[32 + 4 * r : 96 : 16, :].bitcast(I32))
-        scales = [plane[:].bitcast(U8)[:, s * SLICE : (s + 1) * SLICE] for s in range(3)]
+        picked_head = late.tile([P, SCALE_HEAD], U8, name="picked_head", align_bytes=64, offset=3 * ROW - 128)
+        picked_rest = keep.tile([P, S - SCALE_HEAD], U8, name="picked_rest", align_bytes=64)
+        for picked, lo, hi in ((picked_head, 0, SCALE_HEAD), (picked_rest, SCALE_HEAD, S)):
+            nc.vector.tensor_copy(picked[:], scale_win[:].bitcast(U8).indirect(offsets[:, lo // 16 : hi // 16]))
+            for r in range(4):
+                nc.sync.dma_start(plane[r:P:32, lo // 4 : hi // 4], picked[32 + 4 * r : 96 : 16, :].bitcast(I32))
+        planes = [plane[:].bitcast(U8)[:, c : c + SLICE] for c in range(0, S, SLICE)]
 
-        ts_g = [
-            keep.tile([P, SLICE], F32, name="ts_g0", align_bytes=64),
-            late.tile([P, SLICE], F32, name="ts_g1", align_bytes=64, offset=BEHIND - ROW),
-        ]
-        words = [
-            keep.tile([P, SLICE], U32, name="words_even", align_bytes=64),
-            late.tile([P, SLICE], U32, name="words1", align_bytes=64, offset=BEHIND),
-        ]
-
-        def gather_words(s):
-            if s == 2:
-                words.append(keep.tile([P, SLICE], U32, name="words_even", align_bytes=64))
-            nc.vector.tensor_copy(words[s][:], word_win[:].bitcast(U32).indirect(list_slice(s)))
-
-        def gather_ts(s):
-            nc.vector.tensor_copy(ts_g[s][:], ts_win[:].indirect(list_slice(s)))
+        words0 = later.tile([P, SLICE], U32, name="words0", align_bytes=64, offset=2 * STEP)
+        words1 = later.tile([P, SLICE], U32, name="words1", align_bytes=64, offset=7 * STEP)
+        ts_head = keep.tile([P, 2, SLICE], F32, name="ts_head", align_bytes=64)
+        words = [words0[:], words1[:]]
+        ts_g = [ts_head[:, 0, :], ts_head[:, 1, :]]
 
         sums = {}
+        copies = {}
         scaled = {}
 
-        def project(s, m, tokens):
-            y = psum.tile([P, tokens.stop - tokens.start], F32, name="y", tag="bank")
-            for h in range(2):
-                cols = slice(h * M + m * P, h * M + (m + 1) * P)
-                nc.tensor.matmul_mx(
-                    out=y[:],
-                    lhsT=w_codes[:, cols].bitcast(FP8X4),
-                    lhsT_scale=w_scales[:, cols],
-                    rhs=words[s][:, tokens].bitcast(FP8X4),
-                    rhs_scale=scales[s][:, tokens],
-                    start=(h == 0),
-                    stop=(h == 1),
-                )
-            sums[s, m, tokens.start] = y
+        def gather_words(s):
+            nc.vector.tensor_copy(words[s], word_win[:].bitcast(U32).indirect(list_slice(s)))
+            for m in range(2):
+                y = psum.tile([P, SLICE], F32, name="y", tag="bank")
+                for h in range(2):
+                    cols = slice(h * M + m * P, h * M + (m + 1) * P)
+                    nc.tensor.matmul_mx(
+                        out=y[:],
+                        lhsT=w_codes[:, cols].bitcast(FP8X4),
+                        lhsT_scale=w_scales[:, cols],
+                        rhs=words[s].bitcast(FP8X4),
+                        rhs_scale=planes[s],
+                        start=(h == 0),
+                        stop=(h == 1),
+                    )
+                sums[s, m] = y
 
-        def scale_on_gpsimd(s, m, products, place):
-            y_out = late.tile([P, SLICE], F32, name="y_out%d%d" % (s, m), align_bytes=64, offset=BEHIND + place * ROW)
-            z = stage.tile([P, SLICE], F32, name="z")
-            for tokens in (first, second):
-                nc.scalar.activation(y_out[:, tokens], sums[s, m, tokens.start][:], ACT.Copy)
-            for tokens in products:
-                nc.gpsimd.tensor_tensor(z[:, tokens], y_out[:, tokens], ts_g[s][:, tokens], ALU.mult)
+        def gather_ts(s):
+            nc.vector.tensor_copy(ts_g[s], ts_win[:].indirect(list_slice(s)))
+
+        def copy_out(s, m):
+            nc.scalar.activation(copies[s, m], sums[s, m][:], ACT.Copy)
+
+        def copy_tile(s, place):
+            y_out = ring.tile([P, 2, SLICE], F32, name="y_out%d" % s, align_bytes=64, offset=place * ROW)
+            for m in range(2):
+                copies[s, m] = y_out[:, m, :]
+            return y_out
+
+        def scale_half_on_gpsimd(s, m):
+            z = ring.tile([P, SLICE], F32, name="z%d%d" % (s, m), align_bytes=64, offset=(4 + 2 * s + m) * ROW)
+            nc.gpsimd.tensor_tensor(z[:], copies[s, m], ts_g[s], ALU.mult)
             scaled[s, m] = z[:]
 
-        def scale_halves_on_gpsimd(s, m, places):
-            z = stage.tile([P, SLICE], F32, name="z")
-            for tokens, place in zip((first, second), places):
-                y_half = late.tile([P, HALF], F32, name="y_half%d" % place, align_bytes=64, offset=BEHIND + place * ROW)
-                nc.scalar.activation(y_half[:], sums[s, m, 0][:, tokens], ACT.Copy)
-                nc.gpsimd.tensor_tensor(z[:, tokens], y_half[:], ts_g[s][:, tokens], ALU.mult)
-            scaled[s, m] = z[:]
+        def scale_on_gpsimd(s, y_out):
+            z = stage.tile([P, 2, SLICE], F32, name="z")
+            nc.gpsimd.tensor_tensor(z[:], y_out[:], ts_g[s].unsqueeze(1).to_broadcast([P, 2, SLICE]), ALU.mult)
+            for m in range(2):
+                scaled[s, m] = z[:, m, :]
 
-        def scale_on_vector(z, s, m, tokens):
+        def scale_on_vector(z, s, m):
+            nc.vector.tensor_tensor(z, sums[s, m][:], ts_g[s], ALU.mult)
             scaled[s, m] = z
-            nc.vector.tensor_tensor(z[:, tokens], sums[s, m, 0][:, tokens], ts_g[s][:, tokens], ALU.mult)
 
-        def finish(engine, s, m, tokens):
-            result = stage.tile([P, tokens.stop - tokens.start], F32, name="result")
-            z = scaled[s, m][:, tokens]
+        def bias(engine, result, s, m):
             if engine == "scalar":
-                nc.scalar.activation(result[:], z, ACT.Identity, bias=b_col[:, m : m + 1])
-            elif engine == "vector":
-                nc.vector.tensor_scalar(result[:], z, b_col[:, m : m + 1], None, ALU.add)
+                nc.scalar.activation(result, scaled[s, m], ACT.Identity, bias=b_col[:, m : m + 1])
             else:
-                nc.gpsimd.tensor_scalar(result[:], z, 1.0, b_col[:, m : m + 1], ALU.mult, ALU.add)
-            nc.sync.dma_start(out[m * P : (m + 1) * P, s * SLICE + tokens.start : s * SLICE + tokens.stop], result[:])
+                nc.vector.tensor_scalar(result, scaled[s, m], b_col[:, m : m + 1], None, ALU.add)
 
-        whole, first, second = slice(0, SLICE), slice(0, HALF), slice(HALF, SLICE)
+        def store(result, s, m):
+            nc.sync.dma_start(out[m * P : (m + 1) * P, s * SLICE : (s + 1) * SLICE], result)
+
+        def store_both(result, s):
+            nc.sync.dma_start(out.rearrange("(m p) j -> p m j", p=P)[:, :, s * SLICE : (s + 1) * SLICE], result)
+
+        def finish(s, m):
+            result = stage.tile([P, SLICE], F32, name="result_half")
+            bias("scalar", result[:], s, m)
+            store(result[:], s, m)
 
         nc.vector.quantize_mx(
             out=w_codes[:].bitcast(FP8X4), scales=w_scales[:], in_=parts[:].rearrange("p h n t -> p (h n t)")
         )
-        gather_words(0)
-        project(0, 0, first)
-        project(0, 0, second)
-        project(0, 1, first)
-        project(0, 1, second)
-        gather_ts(0)
-        for s in (1, 2):
+        for s in range(2):
             gather_words(s)
-            project(s, 0, whole)
-            project(s, 1, whole)
-            if s == 1:
-                gather_ts(s)
+            gather_ts(s)
+        words2 = late.tile([P, SLICE], U32, name="words2", align_bytes=64, offset=2 * ROW - 64)
+        ts2 = late.tile([P, SLICE], F32, name="ts2", align_bytes=64, offset=3 * ROW + SCALE_HEAD - 192)
+        words.append(words2[:])
+        ts_g.append(ts2[:])
 
-        scale_on_gpsimd(0, 0, (first, second), 1)
-        scale_on_gpsimd(0, 1, (whole,), 3)
-        scale_halves_on_gpsimd(1, 0, (4, 6))
-        finish("scalar", 0, 0, whole)
-        finish("scalar", 0, 1, whole)
+        def declare(s, words_place, ts_place):
+            if words_place is not None:
+                tile = later.tile([P, SLICE], U32, name="words%d" % s, align_bytes=64, offset=words_place * STEP)
+                words.append(tile[:])
+            if ts_place is not None:
+                tile = later.tile([P, SLICE], F32, name="ts%d" % s, align_bytes=64, offset=ts_place * STEP)
+                ts_g.append(tile[:])
 
-        ts_g.append(late.tile([P, SLICE], F32, name="ts_g2", align_bytes=64, offset=BEHIND + ROW // 2))
-        z_mid = late.tile([P, SLICE], F32, name="z_mid", align_bytes=64, offset=BEHIND + 3 * ROW // 2)
-        z_last = late.tile([P, 2, SLICE], F32, name="z_last", align_bytes=64, offset=BEHIND + 4 * ROW)
-
-        scale_on_vector(z_mid[:], 1, 1, whole)
+        gather_words(2)
         gather_ts(2)
-        finish("scalar", 1, 1, whole)
-        finish("scalar", 1, 0, first)
-        finish("gpsimd", 1, 0, second)
-        for tokens in (first, second):
-            scale_on_vector(z_last[:, 0, :], 2, 0, tokens)
-            finish("scalar", 2, 0, tokens)
-        scale_on_vector(z_last[:, 1, :], 2, 1, first)
-        finish("scalar", 2, 1, first)
-        scale_on_vector(z_last[:, 1, :], 2, 1, second)
-        finish("vector", 2, 1, second)
+        declare(3, 1, 3)
+        gather_words(3)
+        gather_ts(3)
+        declare(4, 6, 8)
+        gather_words(4)
+        gather_ts(4)
+        declare(5, 0, None)
+        gather_words(5)
+
+        copy_tile(0, 0)
+        for m in range(2):
+            copy_out(0, m)
+            scale_half_on_gpsimd(0, m)
+        y1 = copy_tile(1, 2)
+        copy_out(1, 0)
+        copy_out(1, 1)
+        scale_on_gpsimd(1, y1)
+        finish(0, 0)
+        finish(0, 1)
+        y2 = copy_tile(2, 0)
+        copy_out(2, 0)
+        copy_out(2, 1)
+        scale_on_gpsimd(2, y2)
+        result1 = late.tile([P, 2, SLICE], F32, name="result1", align_bytes=64, offset=0)
+        for m in range(2):
+            y3 = ring.tile([P, SLICE], F32, name="y_out3%d" % m, align_bytes=64, offset=(2 + m) * ROW)
+            copies[3, m] = y3[:]
+            copy_out(3, m)
+            scale_half_on_gpsimd(3, m)
+            bias("scalar", result1[:, m, :], 1, m)
+        store_both(result1[:], 1)
+        result2 = stage.tile([P, 2, SLICE], F32, name="result")
+        for m in range(2):
+            bias("scalar", result2[:, m, :], 2, m)
+        store_both(result2[:], 2)
+
+        z4 = stage.tile([P, 2, SLICE], F32, name="z")
+        z5 = stage.tile([P, 2, SLICE], F32, name="z")
+        scale_on_vector(z4[:, 0, :], 4, 0)
+        declare(5, None, 5)
+        gather_ts(5)
+        scale_on_vector(z4[:, 1, :], 4, 1)
+        scale_on_vector(z5[:, 0, :], 5, 0)
+        scale_on_vector(z5[:, 1, :], 5, 1)
+        for m in range(2):
+            finish(3, m)
+            result4 = ring.tile([P, SLICE], F32, name="result4%d" % m, align_bytes=64, offset=(2 + m) * ROW)
+            bias("scalar", result4[:], 4, m)
+            store(result4[:], 4, m)
+        result5 = ring.tile([P, 2, SLICE], F32, name="result5", align_bytes=64, offset=11 * ROW)
+        for m in range(2):
+            bias("vector", result5[:, m, :], 5, m)
+        store_both(result5[:], 5)

@@ -259,4 +259,4 @@ def tile_list_tabts_bias_kernel(tc, tab_words, tab_scales, w, ts, b, offs, out):
         result5 = ring.tile([P, 2, SLICE], F32, name="result5", align_bytes=64, offset=11 * ROW)
         for m in range(2):
             bias("vector", result5[:, m, :], 5, m)
-        store_both(result5[:], 5)
+            nc.scalar.dma_start(out[m * P : (m + 1) * P, 5 * SLICE :], result5[:, m, :])

@@ -42,6 +42,7 @@ def tile_list_tabts_bias_kernel(tc, tab_words, tab_scales, w, ts, b, offs, out):
         late = ctx.enter_context(tc.tile_pool(name="late", bufs=1))
         early = ctx.enter_context(tc.tile_pool(name="early", bufs=1))
         later = ctx.enter_context(tc.tile_pool(name="later", bufs=1))
+        soon = ctx.enter_context(tc.tile_pool(name="soon", bufs=1))
         ring = ctx.enter_context(tc.tile_pool(name="ring", bufs=1))
         stage = ctx.enter_context(tc.tile_pool(name="stage", bufs=STAGES))
         psum = ctx.enter_context(tc.psum_pool(name="psum", bufs=BANKS))
@@ -56,7 +57,7 @@ def tile_list_tabts_bias_kernel(tc, tab_words, tab_scales, w, ts, b, offs, out):
 
         zero = early.tile([P, P], I32, name="zero", align_bytes=64, offset=WORD_BYTES - 2 * P)
         nc.vector.memset(zero[:, 0:1], 0)
-        scale_win = keep.tile([P, T // 4], I32, name="scale_win", align_bytes=64)
+        scale_win = soon.tile([P, T // 4], I32, name="scale_win", align_bytes=64, offset=0)
         nc.vector.memset(scale_win[:], 0)
         plane = keep.tile([P, S // 4], I32, name="plane", align_bytes=64)
         nc.vector.tensor_copy(plane[:, :ZERO_COLUMNS], zero[:, 0:1].to_broadcast([P, ZERO_COLUMNS]))
@@ -71,10 +72,6 @@ def tile_list_tabts_bias_kernel(tc, tab_words, tab_scales, w, ts, b, offs, out):
 
         ts_win = early.tile([P, T], F32, name="ts_win", align_bytes=64, offset=WORD_BYTES + BIAS_BYTES)
         nc.sync.dma_start(ts_win[:, TS_HEAD:], ts[:, TS_HEAD:])
-
-        b_col = early.tile([P, M // P], F32, name="b_col", align_bytes=64, offset=WORD_BYTES)
-        with nc.allow_non_contiguous_dma(reason="one bias value to a partition"):
-            nc.sync.dma_start(b_col[:], b.rearrange("(m p) -> p m", p=P))
 
         def list_slice(s):
             return offsets[:, s * (SLICE // 16) : (s + 1) * (SLICE // 16)]
@@ -109,10 +106,21 @@ def tile_list_tabts_bias_kernel(tc, tab_words, tab_scales, w, ts, b, offs, out):
 
         picked_head = late.tile([P, SCALE_HEAD], U8, name="picked_head", align_bytes=64, offset=3 * ROW - 128)
         picked_rest = keep.tile([P, S - SCALE_HEAD], U8, name="picked_rest", align_bytes=64)
-        for picked, lo, hi in ((picked_head, 0, SCALE_HEAD), (picked_rest, SCALE_HEAD, S)):
+        def gather_scales(picked, lo, hi):
             nc.vector.tensor_copy(picked[:], scale_win[:].bitcast(U8).indirect(offsets[:, lo // 16 : hi // 16]))
+
+        def move_scales(picked, lo, hi):
             for r in range(4):
                 nc.sync.dma_start(plane[r:P:32, lo // 4 : hi // 4], picked[32 + 4 * r : 96 : 16, :].bitcast(I32))
+
+        gather_scales(picked_head, 0, SCALE_HEAD)
+        move_scales(picked_head, 0, SCALE_HEAD)
+        gather_scales(picked_rest, SCALE_HEAD, S)
+        b_col = soon.tile([P, M // P], F32, name="b_col", align_bytes=64, offset=0)
+        with nc.allow_non_contiguous_dma(reason="one bias value to a partition"):
+            nc.sync.dma_start(b_col[:], b.rearrange("(m p) -> p m", p=P))
+
+        move_scales(picked_rest, SCALE_HEAD, S)
         planes = [plane[:].bitcast(U8)[:, c : c + SLICE] for c in range(0, S, SLICE)]
 
         words0 = later.tile([P, SLICE], U32, name="words0", align_bytes=64, offset=2 * STEP)

@@ -19,20 +19,27 @@ ACT = mybir.ActivationFunctionType
 P = 128
 PACK = 4
 SLICE = 256
-SCALE_HEAD = 512
+SCALE_HEAD = 2 * SLICE
 HI_MASK = -(1 << 20)
 TS_TAIL = 512
 TS_HEAD = T - TS_TAIL
 RUN = TS_HEAD // P
 QUAD = 4
 CAST_AFTER = 2
+BLOCK = 64
 ROW = 4 * SLICE
-STEP = ROW - 64
+STEP = ROW - BLOCK
 WORD_BYTES = 4 * T
-BIAS_BYTES = 64
-ZERO_COLUMNS = 16
+ZERO_COLUMNS = BLOCK // 4
 STAGES = 6
 BANKS = 8
+
+WORDS_PLACE = {0: 2, 1: 7, 3: 1, 4: 6, 5: 0}
+TS_PLACE = {3: 3, 4: 8, 5: 5}
+
+EVEN_COPIES = 0
+ODD_COPIES = 2
+PRODUCTS = 4
 
 
 def tile_list_tabts_bias_kernel(tc, tab_words, tab_scales, w, ts, b, offs, out):
@@ -49,17 +56,17 @@ def tile_list_tabts_bias_kernel(tc, tab_words, tab_scales, w, ts, b, offs, out):
 
         offsets = keep.tile([P, S // 16], U16, name="offsets")
 
-        w_raw = keep.tile([P, PACK, M], F32, name="w_raw", align_bytes=64)
+        w_raw = keep.tile([P, PACK, M], F32, name="w_raw", align_bytes=BLOCK)
         nc.sync.dma_start(w_raw[:], w.rearrange("(p t) n -> p t n", t=PACK))
         ts_runs = keep.tile([P, RUN], F32, name="ts_runs")
         nc.sync.dma_start(ts_runs[:], ts[0, :TS_HEAD].rearrange("(p c) -> p c", c=RUN))
         nc.sync.dma_start(offsets[:], offs)
 
-        zero = early.tile([P, P], I32, name="zero", align_bytes=64, offset=WORD_BYTES - 2 * P)
+        zero = early.tile([P, P], I32, name="zero", align_bytes=BLOCK, offset=WORD_BYTES - 2 * P)
         nc.vector.memset(zero[:, 0:1], 0)
-        scale_win = soon.tile([P, T // 4], I32, name="scale_win", align_bytes=64, offset=0)
+        scale_win = soon.tile([P, T // 4], I32, name="scale_win", align_bytes=BLOCK, offset=0)
         nc.vector.memset(scale_win[:], 0)
-        plane = keep.tile([P, S // 4], I32, name="plane", align_bytes=64)
+        plane = keep.tile([P, S // 4], I32, name="plane", align_bytes=BLOCK)
         nc.vector.tensor_copy(plane[:, :ZERO_COLUMNS], zero[:, 0:1].to_broadcast([P, ZERO_COLUMNS]))
         nc.vector.memset(plane[:, ZERO_COLUMNS:], 0)
         ident = keep.tile([P, P], F32, name="ident")
@@ -67,19 +74,19 @@ def tile_list_tabts_bias_kernel(tc, tab_words, tab_scales, w, ts, b, offs, out):
 
         nc.sync.dma_start(scale_win[32:96:4, :], tab_scales[0].bitcast(I32))
 
-        word_win = early.tile([P, T], I32, name="word_win", align_bytes=64, offset=0)
+        word_win = early.tile([P, T], I32, name="word_win", align_bytes=BLOCK, offset=0)
         nc.sync.dma_start(word_win[:], tab_words[0].rearrange("p t i -> p (t i)").bitcast(I32))
 
-        ts_win = early.tile([P, T], F32, name="ts_win", align_bytes=64, offset=WORD_BYTES + BIAS_BYTES)
+        ts_win = early.tile([P, T], F32, name="ts_win", align_bytes=BLOCK, offset=WORD_BYTES + BLOCK)
         nc.sync.dma_start(ts_win[:, TS_HEAD:], ts[:, TS_HEAD:])
 
         def list_slice(s):
             return offsets[:, s * (SLICE // 16) : (s + 1) * (SLICE // 16)]
 
-        w_hi = keep.tile([P, M, PACK], I32, name="w_hi", align_bytes=64)
-        parts = keep.tile([P, 2, M, PACK], BF16, name="parts", align_bytes=64)
-        w_codes = keep.tile([P, 2 * M], U32, name="w_codes", align_bytes=64)
-        w_scales = keep.tile([P, 2 * M], U8, name="w_scales", align_bytes=64)
+        w_hi = keep.tile([P, M, PACK], I32, name="w_hi", align_bytes=BLOCK)
+        parts = keep.tile([P, 2, M, PACK], BF16, name="parts", align_bytes=BLOCK)
+        w_codes = keep.tile([P, 2 * M], U32, name="w_codes", align_bytes=BLOCK)
+        w_scales = keep.tile([P, 2 * M], U8, name="w_scales", align_bytes=BLOCK)
 
         nc.vector.tensor_scalar(
             w_hi[:].rearrange("p (c i) t -> p c t i", i=4),
@@ -104,8 +111,12 @@ def tile_list_tabts_bias_kernel(tc, tab_words, tab_scales, w, ts, b, offs, out):
             if q == CAST_AFTER:
                 nc.scalar.activation(parts[:, 0, :, :], w_hi[:].bitcast(F32), ACT.Copy)
 
-        picked_head = late.tile([P, SCALE_HEAD], U8, name="picked_head", align_bytes=64, offset=3 * ROW - 128)
-        picked_rest = keep.tile([P, S - SCALE_HEAD], U8, name="picked_rest", align_bytes=64)
+        words2_at = 2 * ROW - BLOCK
+        picked_at = words2_at + STEP
+        ts2_at = picked_at + SCALE_HEAD - BLOCK
+        picked_head = late.tile([P, SCALE_HEAD], U8, name="picked_head", align_bytes=BLOCK, offset=picked_at)
+        picked_rest = keep.tile([P, S - SCALE_HEAD], U8, name="picked_rest", align_bytes=BLOCK)
+
         def gather_scales(picked, lo, hi):
             nc.vector.tensor_copy(picked[:], scale_win[:].bitcast(U8).indirect(offsets[:, lo // 16 : hi // 16]))
 
@@ -116,24 +127,27 @@ def tile_list_tabts_bias_kernel(tc, tab_words, tab_scales, w, ts, b, offs, out):
         gather_scales(picked_head, 0, SCALE_HEAD)
         move_scales(picked_head, 0, SCALE_HEAD)
         gather_scales(picked_rest, SCALE_HEAD, S)
-        b_col = soon.tile([P, M // P], F32, name="b_col", align_bytes=64, offset=0)
+        b_col = soon.tile([P, M // P], F32, name="b_col", align_bytes=BLOCK, offset=0)
         with nc.allow_non_contiguous_dma(reason="one bias value to a partition"):
             nc.sync.dma_start(b_col[:], b.rearrange("(m p) -> p m", p=P))
-
         move_scales(picked_rest, SCALE_HEAD, S)
-        planes = [plane[:].bitcast(U8)[:, c : c + SLICE] for c in range(0, S, SLICE)]
+        scales = [plane[:].bitcast(U8)[:, c : c + SLICE] for c in range(0, S, SLICE)]
 
-        words0 = later.tile([P, SLICE], U32, name="words0", align_bytes=64, offset=2 * STEP)
-        words1 = later.tile([P, SLICE], U32, name="words1", align_bytes=64, offset=7 * STEP)
-        ts_head = keep.tile([P, 2, SLICE], F32, name="ts_head", align_bytes=64)
-        words = [words0[:], words1[:]]
-        ts_g = [ts_head[:, 0, :], ts_head[:, 1, :]]
-
+        words = {}
+        ts_g = {}
         sums = {}
         copies = {}
         scaled = {}
 
-        def gather_words(s):
+        def place_words(s):
+            tile = later.tile([P, SLICE], U32, name="words%d" % s, align_bytes=BLOCK, offset=WORDS_PLACE[s] * STEP)
+            words[s] = tile[:]
+
+        def place_ts(s):
+            tile = later.tile([P, SLICE], F32, name="ts%d" % s, align_bytes=BLOCK, offset=TS_PLACE[s] * STEP)
+            ts_g[s] = tile[:]
+
+        def gather_and_project(s):
             nc.vector.tensor_copy(words[s], word_win[:].bitcast(U32).indirect(list_slice(s)))
             for m in range(2):
                 y = psum.tile([P, SLICE], F32, name="y", tag="bank")
@@ -144,7 +158,7 @@ def tile_list_tabts_bias_kernel(tc, tab_words, tab_scales, w, ts, b, offs, out):
                         lhsT=w_codes[:, cols].bitcast(FP8X4),
                         lhsT_scale=w_scales[:, cols],
                         rhs=words[s].bitcast(FP8X4),
-                        rhs_scale=planes[s],
+                        rhs_scale=scales[s],
                         start=(h == 0),
                         stop=(h == 1),
                     )
@@ -153,118 +167,106 @@ def tile_list_tabts_bias_kernel(tc, tab_words, tab_scales, w, ts, b, offs, out):
         def gather_ts(s):
             nc.vector.tensor_copy(ts_g[s], ts_win[:].indirect(list_slice(s)))
 
-        def copy_out(s, m):
-            nc.scalar.activation(copies[s, m], sums[s, m][:], ACT.Copy)
-
-        def copy_tile(s, place):
-            y_out = ring.tile([P, 2, SLICE], F32, name="y_out%d" % s, align_bytes=64, offset=place * ROW)
+        def place_copies(s, place):
+            y_out = ring.tile([P, 2, SLICE], F32, name="y_out%d" % s, align_bytes=BLOCK, offset=place * ROW)
             for m in range(2):
                 copies[s, m] = y_out[:, m, :]
             return y_out
 
-        def scale_half_on_gpsimd(s, m):
-            z = ring.tile([P, SLICE], F32, name="z%d%d" % (s, m), align_bytes=64, offset=(4 + 2 * s + m) * ROW)
+        def copy_out(s, m):
+            nc.scalar.activation(copies[s, m], sums[s, m][:], ACT.Copy)
+
+        def scale_tile_on_gpsimd(s, m):
+            place = PRODUCTS + 2 * s + m
+            z = ring.tile([P, SLICE], F32, name="z%d%d" % (s, m), align_bytes=BLOCK, offset=place * ROW)
             nc.gpsimd.tensor_tensor(z[:], copies[s, m], ts_g[s], ALU.mult)
             scaled[s, m] = z[:]
 
-        def scale_on_gpsimd(s, y_out):
+        def scale_slice_on_gpsimd(s, place):
+            y_out = place_copies(s, place)
+            for m in range(2):
+                copy_out(s, m)
             z = stage.tile([P, 2, SLICE], F32, name="z")
             nc.gpsimd.tensor_tensor(z[:], y_out[:], ts_g[s].unsqueeze(1).to_broadcast([P, 2, SLICE]), ALU.mult)
             for m in range(2):
                 scaled[s, m] = z[:, m, :]
 
         def scale_on_vector(z, s, m):
-            nc.vector.tensor_tensor(z, sums[s, m][:], ts_g[s], ALU.mult)
-            scaled[s, m] = z
+            nc.vector.tensor_tensor(z[:, m, :], sums[s, m][:], ts_g[s], ALU.mult)
+            scaled[s, m] = z[:, m, :]
 
-        def bias(engine, result, s, m):
-            if engine == "scalar":
-                nc.scalar.activation(result, scaled[s, m], ACT.Identity, bias=b_col[:, m : m + 1])
-            else:
-                nc.vector.tensor_scalar(result, scaled[s, m], b_col[:, m : m + 1], None, ALU.add)
+        def out_tile(s, m):
+            return out[m * P : (m + 1) * P, s * SLICE : (s + 1) * SLICE]
 
-        def store(result, s, m):
-            nc.sync.dma_start(out[m * P : (m + 1) * P, s * SLICE : (s + 1) * SLICE], result)
-
-        def store_both(result, s):
-            nc.sync.dma_start(out.rearrange("(m p) j -> p m j", p=P)[:, :, s * SLICE : (s + 1) * SLICE], result)
+        def bias_on_scalar(result, s, m):
+            nc.scalar.activation(result, scaled[s, m], ACT.Identity, bias=b_col[:, m : m + 1])
 
         def finish(s, m):
             result = stage.tile([P, SLICE], F32, name="result_half")
-            bias("scalar", result[:], s, m)
-            store(result[:], s, m)
+            bias_on_scalar(result[:], s, m)
+            nc.sync.dma_start(out_tile(s, m), result[:])
 
+        place_words(0)
+        place_words(1)
+        ts_head = keep.tile([P, 2, SLICE], F32, name="ts_head", align_bytes=BLOCK)
         nc.vector.quantize_mx(
             out=w_codes[:].bitcast(FP8X4), scales=w_scales[:], in_=parts[:].rearrange("p h n t -> p (h n t)")
         )
         for s in range(2):
-            gather_words(s)
+            ts_g[s] = ts_head[:, s, :]
+            gather_and_project(s)
             gather_ts(s)
-        words2 = late.tile([P, SLICE], U32, name="words2", align_bytes=64, offset=2 * ROW - 64)
-        ts2 = late.tile([P, SLICE], F32, name="ts2", align_bytes=64, offset=3 * ROW + SCALE_HEAD - 192)
-        words.append(words2[:])
-        ts_g.append(ts2[:])
-
-        def declare(s, words_place, ts_place):
-            if words_place is not None:
-                tile = later.tile([P, SLICE], U32, name="words%d" % s, align_bytes=64, offset=words_place * STEP)
-                words.append(tile[:])
-            if ts_place is not None:
-                tile = later.tile([P, SLICE], F32, name="ts%d" % s, align_bytes=64, offset=ts_place * STEP)
-                ts_g.append(tile[:])
-
-        gather_words(2)
+        words2 = late.tile([P, SLICE], U32, name="words2", align_bytes=BLOCK, offset=words2_at)
+        ts2 = late.tile([P, SLICE], F32, name="ts2", align_bytes=BLOCK, offset=ts2_at)
+        words[2] = words2[:]
+        ts_g[2] = ts2[:]
+        gather_and_project(2)
         gather_ts(2)
-        declare(3, 1, 3)
-        gather_words(3)
-        gather_ts(3)
-        declare(4, 6, 8)
-        gather_words(4)
-        gather_ts(4)
-        declare(5, 0, None)
-        gather_words(5)
+        for s in (3, 4):
+            place_words(s)
+            place_ts(s)
+            gather_and_project(s)
+            gather_ts(s)
+        place_words(5)
+        gather_and_project(5)
 
-        copy_tile(0, 0)
+        place_copies(0, EVEN_COPIES)
         for m in range(2):
             copy_out(0, m)
-            scale_half_on_gpsimd(0, m)
-        y1 = copy_tile(1, 2)
-        copy_out(1, 0)
-        copy_out(1, 1)
-        scale_on_gpsimd(1, y1)
-        finish(0, 0)
-        finish(0, 1)
-        y2 = copy_tile(2, 0)
-        copy_out(2, 0)
-        copy_out(2, 1)
-        scale_on_gpsimd(2, y2)
-        result1 = late.tile([P, 2, SLICE], F32, name="result1", align_bytes=64, offset=0)
+            scale_tile_on_gpsimd(0, m)
+        scale_slice_on_gpsimd(1, ODD_COPIES)
         for m in range(2):
-            y3 = ring.tile([P, SLICE], F32, name="y_out3%d" % m, align_bytes=64, offset=(2 + m) * ROW)
+            finish(0, m)
+        scale_slice_on_gpsimd(2, EVEN_COPIES)
+        result1 = late.tile([P, 2, SLICE], F32, name="result1", align_bytes=BLOCK, offset=0)
+        for m in range(2):
+            y3 = ring.tile([P, SLICE], F32, name="y_out3%d" % m, align_bytes=BLOCK, offset=(ODD_COPIES + m) * ROW)
             copies[3, m] = y3[:]
             copy_out(3, m)
-            scale_half_on_gpsimd(3, m)
-            bias("scalar", result1[:, m, :], 1, m)
-        store_both(result1[:], 1)
-        result2 = stage.tile([P, 2, SLICE], F32, name="result")
+            scale_tile_on_gpsimd(3, m)
+            bias_on_scalar(result1[:, m, :], 1, m)
+            nc.sync.dma_start(out_tile(1, m), result1[:, m, :])
         for m in range(2):
-            bias("scalar", result2[:, m, :], 2, m)
-        store_both(result2[:], 2)
+            finish(2, m)
 
         z4 = stage.tile([P, 2, SLICE], F32, name="z")
         z5 = stage.tile([P, 2, SLICE], F32, name="z")
-        scale_on_vector(z4[:, 0, :], 4, 0)
-        declare(5, None, 5)
+        scale_on_vector(z4, 4, 0)
+        place_ts(5)
         gather_ts(5)
-        scale_on_vector(z4[:, 1, :], 4, 1)
-        scale_on_vector(z5[:, 0, :], 5, 0)
-        scale_on_vector(z5[:, 1, :], 5, 1)
+        scale_on_vector(z4, 4, 1)
+        scale_on_vector(z5, 5, 0)
+        scale_on_vector(z5, 5, 1)
+
         for m in range(2):
             finish(3, m)
-            result4 = ring.tile([P, SLICE], F32, name="result4%d" % m, align_bytes=64, offset=(2 + m) * ROW)
-            bias("scalar", result4[:], 4, m)
-            store(result4[:], 4, m)
-        result5 = ring.tile([P, 2, SLICE], F32, name="result5", align_bytes=64, offset=11 * ROW)
+            place = ODD_COPIES + m
+            result4 = ring.tile([P, SLICE], F32, name="result4%d" % m, align_bytes=BLOCK, offset=place * ROW)
+            bias_on_scalar(result4[:], 4, m)
+            nc.sync.dma_start(out_tile(4, m), result4[:])
+
+        place = PRODUCTS + 2 * 3 + 1
+        result5 = ring.tile([P, 2, SLICE], F32, name="result5", align_bytes=BLOCK, offset=place * ROW)
         for m in range(2):
-            bias("vector", result5[:, m, :], 5, m)
-            nc.scalar.dma_start(out[m * P : (m + 1) * P, 5 * SLICE :], result5[:, m, :])
+            nc.vector.tensor_scalar(result5[:, m, :], scaled[5, m], b_col[:, m : m + 1], None, ALU.add)
+            nc.scalar.dma_start(out_tile(5, m), result5[:, m, :])

from contextlib import ExitStack

import concourse.mybir as mybir
from concourse.masks import make_identity

K, M, T, S = 512, 256, 4096, 1536
FLOPS = 2 * 2 * K * M * S

F32 = mybir.dt.float32
BF16 = mybir.dt.bfloat16
I32 = mybir.dt.int32
U32 = mybir.dt.uint32
U16 = mybir.dt.uint16
U8 = mybir.dt.uint8
FP8X4 = mybir.dt.float8_e4m3fn_x4
ALU = mybir.AluOpType
ACT = mybir.ActivationFunctionType

P = 128
PACK = 4
SLICE = 256
SCALE_HEAD = 2 * SLICE
HI_MASK = -(1 << 20)
TS_TAIL = 512
TS_HEAD = T - TS_TAIL
RUN = TS_HEAD // P
QUAD = 4
CAST_AFTER = 2
BLOCK = 64
ROW = 4 * SLICE
STEP = ROW - BLOCK
WORD_BYTES = 4 * T
ZERO_COLUMNS = BLOCK // 4
STAGES = 6
BANKS = 8

WORDS_PLACE = {0: 2, 1: 7, 3: 1, 4: 6, 5: 0}
TS_PLACE = {3: 3, 4: 8, 5: 5}

EVEN_COPIES = 0
ODD_COPIES = 2
PRODUCTS = 4


def tile_list_tabts_bias_kernel(tc, tab_words, tab_scales, w, ts, b, offs, out):
    nc = tc.nc
    with ExitStack() as ctx:
        keep = ctx.enter_context(tc.tile_pool(name="keep", bufs=1))
        late = ctx.enter_context(tc.tile_pool(name="late", bufs=1))
        early = ctx.enter_context(tc.tile_pool(name="early", bufs=1))
        later = ctx.enter_context(tc.tile_pool(name="later", bufs=1))
        soon = ctx.enter_context(tc.tile_pool(name="soon", bufs=1))
        ring = ctx.enter_context(tc.tile_pool(name="ring", bufs=1))
        stage = ctx.enter_context(tc.tile_pool(name="stage", bufs=STAGES))
        psum = ctx.enter_context(tc.psum_pool(name="psum", bufs=BANKS))

        offsets = keep.tile([P, S // 16], U16, name="offsets")

        w_raw = keep.tile([P, PACK, M], F32, name="w_raw", align_bytes=BLOCK)
        nc.sync.dma_start(w_raw[:], w.rearrange("(p t) n -> p t n", t=PACK))
        ts_runs = keep.tile([P, RUN], F32, name="ts_runs")
        nc.sync.dma_start(ts_runs[:], ts[0, :TS_HEAD].rearrange("(p c) -> p c", c=RUN))
        nc.sync.dma_start(offsets[:], offs)

        zero = early.tile([P, P], I32, name="zero", align_bytes=BLOCK, offset=WORD_BYTES - 2 * P)
        nc.vector.memset(zero[:, 0:1], 0)
        scale_win = soon.tile([P, T // 4], I32, name="scale_win", align_bytes=BLOCK, offset=0)
        nc.vector.memset(scale_win[:], 0)
        plane = keep.tile([P, S // 4], I32, name="plane", align_bytes=BLOCK)
        nc.vector.tensor_copy(plane[:, :ZERO_COLUMNS], zero[:, 0:1].to_broadcast([P, ZERO_COLUMNS]))
        nc.vector.memset(plane[:, ZERO_COLUMNS:], 0)
        ident = keep.tile([P, P], F32, name="ident")
        make_identity(nc, ident[:])

        nc.sync.dma_start(scale_win[32:96:4, :], tab_scales[0].bitcast(I32))

        word_win = early.tile([P, T], I32, name="word_win", align_bytes=BLOCK, offset=0)
        nc.sync.dma_start(word_win[:], tab_words[0].rearrange("p t i -> p (t i)").bitcast(I32))

        ts_win = early.tile([P, T], F32, name="ts_win", align_bytes=BLOCK, offset=WORD_BYTES + BLOCK)
        nc.sync.dma_start(ts_win[:, TS_HEAD:], ts[:, TS_HEAD:])

        def list_slice(s):
            return offsets[:, s * (SLICE // 16) : (s + 1) * (SLICE // 16)]

        w_hi = keep.tile([P, M, PACK], I32, name="w_hi", align_bytes=BLOCK)
        parts = keep.tile([P, 2, M, PACK], BF16, name="parts", align_bytes=BLOCK)
        w_codes = keep.tile([P, 2 * M], U32, name="w_codes", align_bytes=BLOCK)
        w_scales = keep.tile([P, 2 * M], U8, name="w_scales", align_bytes=BLOCK)

        nc.vector.tensor_scalar(
            w_hi[:].rearrange("p (c i) t -> p c t i", i=4),
            w_raw[:].bitcast(I32).rearrange("p t (c i) -> p c t i", i=4),
            HI_MASK,
            None,
            ALU.bitwise_and,
        )
        nc.gpsimd.tensor_tensor(
            parts[:, 1, :, :], w_raw[:].rearrange("p t n -> p n t"), w_hi[:].bitcast(F32), ALU.subtract
        )

        ts_cells = ts_win[:, :TS_HEAD].rearrange("m (p c) -> m p c", c=RUN)
        for q in range(RUN // QUAD):
            spread = psum.tile([P, QUAD, P], F32, name="spread", tag="bank")
            for i in range(QUAD):
                c = q * QUAD + i
                nc.tensor.transpose(spread[:, i, :], ts_runs[:, c : c + 1].to_broadcast([P, P]), ident[:])
            nc.scalar.activation(
                ts_cells[:, :, q * QUAD : (q + 1) * QUAD], spread[:].rearrange("m c p -> m p c"), ACT.Copy
            )
            if q == CAST_AFTER:
                nc.scalar.activation(parts[:, 0, :, :], w_hi[:].bitcast(F32), ACT.Copy)

        words2_at = 2 * ROW - BLOCK
        picked_at = words2_at + STEP
        ts2_at = picked_at + SCALE_HEAD - BLOCK
        picked_head = late.tile([P, SCALE_HEAD], U8, name="picked_head", align_bytes=BLOCK, offset=picked_at)
        picked_rest = keep.tile([P, S - SCALE_HEAD], U8, name="picked_rest", align_bytes=BLOCK)

        def gather_scales(picked, lo, hi):
            nc.vector.tensor_copy(picked[:], scale_win[:].bitcast(U8).indirect(offsets[:, lo // 16 : hi // 16]))

        def move_scales(picked, lo, hi):
            for r in range(4):
                nc.sync.dma_start(plane[r:P:32, lo // 4 : hi // 4], picked[32 + 4 * r : 96 : 16, :].bitcast(I32))

        gather_scales(picked_head, 0, SCALE_HEAD)
        move_scales(picked_head, 0, SCALE_HEAD)
        gather_scales(picked_rest, SCALE_HEAD, S)
        b_col = soon.tile([P, M // P], F32, name="b_col", align_bytes=BLOCK, offset=0)
        with nc.allow_non_contiguous_dma(reason="one bias value to a partition"):
            nc.sync.dma_start(b_col[:], b.rearrange("(m p) -> p m", p=P))
        move_scales(picked_rest, SCALE_HEAD, S)
        scales = [plane[:].bitcast(U8)[:, c : c + SLICE] for c in range(0, S, SLICE)]

        words = {}
        ts_g = {}
        sums = {}
        copies = {}
        scaled = {}

        def place_words(s):
            tile = later.tile([P, SLICE], U32, name="words%d" % s, align_bytes=BLOCK, offset=WORDS_PLACE[s] * STEP)
            words[s] = tile[:]

        def place_ts(s):
            tile = later.tile([P, SLICE], F32, name="ts%d" % s, align_bytes=BLOCK, offset=TS_PLACE[s] * STEP)
            ts_g[s] = tile[:]

        def gather_and_project(s):
            nc.vector.tensor_copy(words[s], word_win[:].bitcast(U32).indirect(list_slice(s)))
            for m in range(2):
                y = psum.tile([P, SLICE], F32, name="y", tag="bank")
                for h in range(2):
                    cols = slice(h * M + m * P, h * M + (m + 1) * P)
                    nc.tensor.matmul_mx(
                        out=y[:],
                        lhsT=w_codes[:, cols].bitcast(FP8X4),
                        lhsT_scale=w_scales[:, cols],
                        rhs=words[s].bitcast(FP8X4),
                        rhs_scale=scales[s],
                        start=(h == 0),
                        stop=(h == 1),
                    )
                sums[s, m] = y

        def gather_ts(s):
            nc.vector.tensor_copy(ts_g[s], ts_win[:].indirect(list_slice(s)))

        def place_copies(s, place):
            y_out = ring.tile([P, 2, SLICE], F32, name="y_out%d" % s, align_bytes=BLOCK, offset=place * ROW)
            for m in range(2):
                copies[s, m] = y_out[:, m, :]
            return y_out

        def copy_out(s, m):
            nc.scalar.activation(copies[s, m], sums[s, m][:], ACT.Copy)

        def scale_tile_on_gpsimd(s, m):
            place = PRODUCTS + 2 * s + m
            z = ring.tile([P, SLICE], F32, name="z%d%d" % (s, m), align_bytes=BLOCK, offset=place * ROW)
            nc.gpsimd.tensor_tensor(z[:], copies[s, m], ts_g[s], ALU.mult)
            scaled[s, m] = z[:]

        def scale_slice_on_gpsimd(s, place):
            y_out = place_copies(s, place)
            for m in range(2):
                copy_out(s, m)
            z = stage.tile([P, 2, SLICE], F32, name="z")
            nc.gpsimd.tensor_tensor(z[:], y_out[:], ts_g[s].unsqueeze(1).to_broadcast([P, 2, SLICE]), ALU.mult)
            for m in range(2):
                scaled[s, m] = z[:, m, :]

        def scale_on_vector(z, s, m):
            nc.vector.tensor_tensor(z[:, m, :], sums[s, m][:], ts_g[s], ALU.mult)
            scaled[s, m] = z[:, m, :]

        def out_tile(s, m):
            return out[m * P : (m + 1) * P, s * SLICE : (s + 1) * SLICE]

        def bias_on_scalar(result, s, m):
            nc.scalar.activation(result, scaled[s, m], ACT.Identity, bias=b_col[:, m : m + 1])

        def finish(s, m):
            result = stage.tile([P, SLICE], F32, name="result_half")
            bias_on_scalar(result[:], s, m)
            nc.sync.dma_start(out_tile(s, m), result[:])

        place_words(0)
        place_words(1)
        ts_head = keep.tile([P, 2, SLICE], F32, name="ts_head", align_bytes=BLOCK)
        nc.vector.quantize_mx(
            out=w_codes[:].bitcast(FP8X4), scales=w_scales[:], in_=parts[:].rearrange("p h n t -> p (h n t)")
        )
        for s in range(2):
            ts_g[s] = ts_head[:, s, :]
            gather_and_project(s)
            gather_ts(s)
        words2 = late.tile([P, SLICE], U32, name="words2", align_bytes=BLOCK, offset=words2_at)
        ts2 = late.tile([P, SLICE], F32, name="ts2", align_bytes=BLOCK, offset=ts2_at)
        words[2] = words2[:]
        ts_g[2] = ts2[:]
        gather_and_project(2)
        gather_ts(2)
        for s in (3, 4):
            place_words(s)
            place_ts(s)
            gather_and_project(s)
            gather_ts(s)
        place_words(5)
        gather_and_project(5)

        place_copies(0, EVEN_COPIES)
        for m in range(2):
            copy_out(0, m)
            scale_tile_on_gpsimd(0, m)
        scale_slice_on_gpsimd(1, ODD_COPIES)
        for m in range(2):
            finish(0, m)
        scale_slice_on_gpsimd(2, EVEN_COPIES)
        result1 = late.tile([P, 2, SLICE], F32, name="result1", align_bytes=BLOCK, offset=0)
        for m in range(2):
            y3 = ring.tile([P, SLICE], F32, name="y_out3%d" % m, align_bytes=BLOCK, offset=(ODD_COPIES + m) * ROW)
            copies[3, m] = y3[:]
            copy_out(3, m)
            scale_tile_on_gpsimd(3, m)
            bias_on_scalar(result1[:, m, :], 1, m)
            nc.sync.dma_start(out_tile(1, m), result1[:, m, :])
        for m in range(2):
            finish(2, m)

        z4 = stage.tile([P, 2, SLICE], F32, name="z")
        z5 = stage.tile([P, 2, SLICE], F32, name="z")
        scale_on_vector(z4, 4, 0)
        place_ts(5)
        gather_ts(5)
        scale_on_vector(z4, 4, 1)
        scale_on_vector(z5, 5, 0)
        scale_on_vector(z5, 5, 1)

        for m in range(2):
            finish(3, m)
            place = ODD_COPIES + m
            result4 = ring.tile([P, SLICE], F32, name="result4%d" % m, align_bytes=BLOCK, offset=place * ROW)
            bias_on_scalar(result4[:], 4, m)
            nc.sync.dma_start(out_tile(4, m), result4[:])

        place = PRODUCTS + 2 * 3 + 1
        result5 = ring.tile([P, 2, SLICE], F32, name="result5", align_bytes=BLOCK, offset=place * ROW)
        for m in range(2):
            nc.vector.tensor_scalar(result5[:, m, :], scaled[5, m], b_col[:, m : m + 1], None, ALU.add)
            nc.scalar.dma_start(out_tile(5, m), result5[:, m, :])
